import numpy as np
import ml_dtypes


def mxq(x, axis, fmt="e4m3"):
    dtype, down = {"e4m3": (ml_dtypes.float8_e4m3fn, 7), "e5m2": (ml_dtypes.float8_e5m2, 14)}[fmt]
    v = np.moveaxis(np.asarray(x, np.float32).astype(ml_dtypes.bfloat16).astype(np.float64), axis, -1)
    blocks = v.reshape(v.shape[:-1] + (-1, 32))
    amax = np.abs(blocks).max(-1, keepdims=True)
    byte = np.maximum(np.where(amax > 0, np.frexp(amax)[1] - 1 + 127, 0) - down, 1)
    scale = np.exp2(byte - 127.0)
    codes = (blocks / scale).astype(np.float32).astype(dtype).astype(np.float64)
    return np.moveaxis((codes * scale).reshape(v.shape), -1, axis)


WIDE = False


def mx_kscale(k):
    if not WIDE:
        return np.ones(k)
    levels = np.array([18, -18])
    if k % 512:
        return np.exp2(np.random.permutation(np.resize(levels, k // 32))).repeat(32)
    a = np.empty((k // 512, 16))
    for p in range(k // 512):
        a[p, :8] = np.random.permutation(np.resize(levels, 8))
        for g in range(8):
            far = levels[np.abs(levels - a[p, g]) >= 10]
            a[p, g + 8] = far[np.random.randint(len(far))]
    return np.exp2(a.ravel()).repeat(32)


def f64(x):
    return np.asarray(x).astype(np.float64)


def striped(idx):
    return np.tile(np.asarray(idx).reshape(-1, 16).T, (8, 1)).astype(np.uint16)


def unstriped(offs):
    return offs[:16].T.reshape(-1).astype(np.int64)


def setup_inputs():
    n = np.random.standard_normal
    uni = np.random.uniform
    idx = np.random.permutation(2048)[:512]
    jdx = np.random.permutation(1024)[:512]
    f_f = mx_kscale(512)
    return {
        "aT": (n((512, 2048))).astype(np.float32),
        "bT": (n((512, 1024))).astype(np.float32),
        "W": (n((512, 512)) / np.sqrt(512) * f_f[:, None]).astype(np.float32),
        "dz": (n((512, 512)) / f_f[:, None]).astype(np.float32),
        "offs": striped(idx),
        "joffs": striped(jdx),
    }


def reference(aT, bT, W, dz, offs, joffs):
    idx = unstriped(offs)
    jdx = unstriped(joffs)
    a_ = f64(aT)[:, idx]
    b_ = f64(bT)[:, jdx]
    de = mxq(f64(W), 0, "e4m3").T @ mxq(f64(dz), 0, "e5m2")
    da = de * b_
    out_0 = np.zeros((512, 2048))
    out_0[:, idx] = da
    db = de * a_
    out_1 = np.zeros((512, 1024))
    out_1[:, jdx] = db
    return out_0, out_1

@@ -1,0 +1,112 @@
+from contextlib import ExitStack
+
+import concourse.mybir as mybir
+
+D, F, ITEMS, A_COLS, B_COLS = 512, 512, 512, 2048, 1024
+FLOPS = 2 * D * F * ITEMS
+
+F32 = mybir.dt.float32
+BF16 = mybir.dt.bfloat16
+U32 = mybir.dt.uint32
+U16 = mybir.dt.uint16
+U8 = mybir.dt.uint8
+E4M3X4 = mybir.dt.float8_e4m3fn_x4
+E5M2X4 = mybir.dt.float8_e5m2_x4
+MULT = mybir.AluOpType.mult
+
+P = 128
+PACK = 4
+D_TILES = D // P
+HALF = ITEMS // 2
+WINDOWS = 2
+
+
+def interleave(copy, grouped, raw):
+    copy(
+        out=grouped.rearrange("p (c i t) -> p c t i", i=PACK, t=PACK),
+        in_=raw.rearrange("p t (c i) -> p c t i", i=PACK),
+    )
+
+
+def tile_attend_gqr_ab_kernel(tc, aT, bT, W, dz, offs, joffs, out_0, out_1):
+    nc = tc.nc
+    with ExitStack() as ctx:
+        keep = ctx.enter_context(tc.tile_pool(name="keep", bufs=1))
+        psum = ctx.enter_context(tc.psum_pool(name="psum", bufs=1))
+
+        a_list = keep.tile([P, ITEMS // 16], U16, name="a_list")
+        b_list = keep.tile([P, ITEMS // 16], U16, name="b_list")
+        dz_raw = [keep.tile([P, PACK, HALF], F32, name=f"dz_raw{h}") for h in range(2)]
+        w_first = keep.tile([P, PACK, P], F32, name="w_first")
+        w_rest = keep.tile([P, PACK, D - P], F32, name="w_rest")
+        a_tab = [keep.tile([P, A_COLS], F32, name=f"a_tab{t}") for t in range(D_TILES)]
+        b_tab = [keep.tile([P, B_COLS], F32, name=f"b_tab{t}") for t in range(D_TILES)]
+        win_0 = [keep.tile([P, A_COLS], F32, name=f"win_0_{w}") for w in range(WINDOWS)]
+        win_1 = [keep.tile([P, B_COLS], F32, name=f"win_1_{w}") for w in range(WINDOWS)]
+        dz_bf = [keep.tile([P, HALF * PACK], BF16, name=f"dz_bf{h}", align_bytes=64) for h in range(2)]
+        w_bf = [keep.tile([P, P * PACK], BF16, name=f"w_bf{t}", align_bytes=64) for t in range(D_TILES)]
+        dz_codes = keep.tile([P, ITEMS], U32, name="dz_codes", align_bytes=64)
+        dz_scales = keep.tile([P, ITEMS], U8, name="dz_scales", align_bytes=64)
+        w_codes = [keep.tile([P, P], U32, name=f"w_codes{t}", align_bytes=64) for t in range(D_TILES)]
+        w_scales = [keep.tile([P, P], U8, name=f"w_scales{t}", align_bytes=64) for t in range(D_TILES)]
+        de = [keep.tile([P, ITEMS], F32, name=f"de{t}") for t in range(D_TILES)]
+        a_got = [keep.tile([P, ITEMS], F32, name=f"a_got{t}") for t in range(D_TILES)]
+        b_got = [keep.tile([P, ITEMS], F32, name=f"b_got{t}") for t in range(D_TILES)]
+        de_psum = [psum.tile([P, ITEMS], F32, name=f"de_psum{t}") for t in range(D_TILES)]
+
+        dz_rows = dz.rearrange("(p t) i -> p t i", t=PACK)
+        w_rows = W.rearrange("(p t) d -> p t d", t=PACK)
+
+        def rows(t):
+            return slice(t * P, (t + 1) * P)
+
+        for h in range(2):
+            nc.sync.dma_start(out=dz_raw[h][:], in_=dz_rows[:, :, h * HALF : (h + 1) * HALF])
+        nc.sync.dma_start(out=w_first[:], in_=w_rows[:, :, 0:P])
+        nc.sync.dma_start(b_list[:], joffs)
+        nc.sync.dma_start(out=b_tab[0][:], in_=bT[rows(0), :])
+        nc.sync.dma_start(a_list[:], offs)
+        nc.sync.dma_start(out=a_tab[0][:], in_=aT[rows(0), :])
+        nc.sync.dma_start(out=w_rest[:], in_=w_rows[:, :, P:D])
+        for t in range(1, D_TILES):
+            nc.sync.dma_start(out=b_tab[t][:], in_=bT[rows(t), :])
+            nc.sync.dma_start(out=a_tab[t][:], in_=aT[rows(t), :])
+
+        for w in range(WINDOWS):
+            nc.vector.memset(win_0[w][:], 0.0)
+            nc.vector.memset(win_1[w][:], 0.0)
+
+        interleave(nc.scalar.copy, dz_bf[0][:], dz_raw[0][:])
+        interleave(nc.vector.tensor_copy, dz_bf[1][:], dz_raw[1][:])
+        interleave(nc.scalar.copy, w_bf[0][:], w_first[:])
+        for h in range(2):
+            items = slice(h * HALF, (h + 1) * HALF)
+            nc.vector.quantize_mx(out=dz_codes[:, items].bitcast(E5M2X4), scales=dz_scales[:, items], in_=dz_bf[h][:])
+
+        def make_de(t):
+            nc.vector.quantize_mx(out=w_codes[t][:].bitcast(E4M3X4), scales=w_scales[t][:], in_=w_bf[t][:])
+            nc.tensor.matmul_mx(
+                out=de_psum[t][:],
+                lhsT=w_codes[t][:].bitcast(E4M3X4),
+                lhsT_scale=w_scales[t][:],
+                rhs=dz_codes[:].bitcast(E5M2X4),
+                rhs_scale=dz_scales[:],
+                start=True,
+                stop=True,
+            )
+            nc.scalar.copy(out=de[t][:], in_=de_psum[t][:])
+
+        make_de(0)
+        for t in range(1, D_TILES):
+            interleave(nc.scalar.copy, w_bf[t][:], w_rest[:, :, (t - 1) * P : t * P])
+
+        for t in range(D_TILES):
+            w0, w1 = win_0[t % WINDOWS], win_1[t % WINDOWS]
+            nc.vector.tensor_copy(b_got[t][:], b_tab[t][:].indirect(b_list[:]))
+            nc.vector.tensor_tensor(w0[:].indirect(a_list[:]), de[t][:], b_got[t][:], MULT)
+            nc.sync.dma_start(out=out_0[rows(t), :], in_=w0[:])
+            if t + 1 < D_TILES:
+                make_de(t + 1)
+            nc.vector.tensor_copy(a_got[t][:], a_tab[t][:].indirect(a_list[:]))
+            nc.vector.tensor_tensor(w1[:].indirect(b_list[:]), de[t][:], a_got[t][:], MULT)
+            nc.sync.dma_start(out=out_1[rows(t), :], in_=w1[:])

@@ -8,6 +8,7 @@ FLOPS = 2 * D * F * ITEMS
 F32 = mybir.dt.float32
 BF16 = mybir.dt.bfloat16
 U32 = mybir.dt.uint32
+I32 = mybir.dt.int32
 U16 = mybir.dt.uint16
 U8 = mybir.dt.uint8
 E4M3X4 = mybir.dt.float8_e4m3fn_x4
@@ -39,7 +40,7 @@ def tile_attend_gqr_ab_kernel(tc, aT, bT, W, dz, offs, joffs, out_0, out_1):
         dz_raw = [keep.tile([P, PACK, HALF], F32, name=f"dz_raw{h}") for h in range(2)]
         w_first = keep.tile([P, PACK, P], F32, name="w_first")
         w_rest = keep.tile([P, PACK, D - P], F32, name="w_rest")
-        a_tab = [keep.tile([P, A_COLS], F32, name=f"a_tab{t}") for t in range(D_TILES)]
+        a_pair = [keep.tile([P, 2, A_COLS], F32, name=f"a_pair{g}") for g in range(D_TILES // 2)]
         b_tab = [keep.tile([P, B_COLS], F32, name=f"b_tab{t}") for t in range(D_TILES)]
         win_0 = [keep.tile([P, A_COLS], F32, name=f"win_0_{w}") for w in range(WINDOWS)]
         win_1 = [keep.tile([P, B_COLS], F32, name=f"win_1_{w}") for w in range(WINDOWS)]
@@ -66,15 +67,16 @@ def tile_attend_gqr_ab_kernel(tc, aT, bT, W, dz, offs, joffs, out_0, out_1):
         nc.sync.dma_start(b_list[:], joffs)
         nc.sync.dma_start(out=b_tab[0][:], in_=bT[rows(0), :])
         nc.sync.dma_start(a_list[:], offs)
-        nc.sync.dma_start(out=a_tab[0][:], in_=aT[rows(0), :])
+        nc.sync.dma_start(out=b_tab[1][:], in_=bT[rows(1), :])
         nc.sync.dma_start(out=w_rest[:], in_=w_rows[:, :, P:D])
-        for t in range(1, D_TILES):
-            nc.sync.dma_start(out=b_tab[t][:], in_=bT[rows(t), :])
-            nc.sync.dma_start(out=a_tab[t][:], in_=aT[rows(t), :])
+        nc.sync.dma_start(out=b_tab[2][:], in_=bT[rows(2), :])
+        nc.sync.dma_start(out=a_pair[0][:], in_=aT[0 : 2 * P, :].rearrange("(u p) c -> p u c", p=P))
+        nc.sync.dma_start(out=b_tab[3][:], in_=bT[rows(3), :])
+        nc.sync.dma_start(out=a_pair[1][:], in_=aT[2 * P : 4 * P, :].rearrange("(u p) c -> p u c", p=P))
 
         for w in range(WINDOWS):
-            nc.vector.memset(win_0[w][:], 0.0)
-            nc.vector.memset(win_1[w][:], 0.0)
+            nc.vector.memset(win_0[w][:].bitcast(I32), 0)
+            nc.vector.memset(win_1[w][:].bitcast(I32), 0)
 
         interleave(nc.scalar.copy, dz_bf[0][:], dz_raw[0][:])
         interleave(nc.vector.tensor_copy, dz_bf[1][:], dz_raw[1][:])
@@ -100,13 +102,38 @@ def tile_attend_gqr_ab_kernel(tc, aT, bT, W, dz, offs, joffs, out_0, out_1):
         for t in range(1, D_TILES):
             interleave(nc.scalar.copy, w_bf[t][:], w_rest[:, :, (t - 1) * P : t * P])
 
-        for t in range(D_TILES):
-            w0, w1 = win_0[t % WINDOWS], win_1[t % WINDOWS]
+        def gather_a(t):
+            nc.vector.tensor_copy(a_got[t][:], a_pair[t // 2][:, t % 2, :].indirect(a_list[:]))
+
+        def gather_b(t):
             nc.vector.tensor_copy(b_got[t][:], b_tab[t][:].indirect(b_list[:]))
-            nc.vector.tensor_tensor(w0[:].indirect(a_list[:]), de[t][:], b_got[t][:], MULT)
-            nc.sync.dma_start(out=out_0[rows(t), :], in_=w0[:])
-            if t + 1 < D_TILES:
-                make_de(t + 1)
-            nc.vector.tensor_copy(a_got[t][:], a_tab[t][:].indirect(a_list[:]))
-            nc.vector.tensor_tensor(w1[:].indirect(b_list[:]), de[t][:], a_got[t][:], MULT)
-            nc.sync.dma_start(out=out_1[rows(t), :], in_=w1[:])
+
+        def scatter_0(t):
+            window = win_0[t % WINDOWS]
+            nc.vector.tensor_tensor(window[:].indirect(a_list[:]), de[t][:], b_got[t][:], MULT)
+            nc.sync.dma_start(out=out_0[rows(t), :], in_=window[:])
+
+        def scatter_1(t):
+            window = win_1[t % WINDOWS]
+            nc.vector.tensor_tensor(window[:].indirect(b_list[:]), de[t][:], a_got[t][:], MULT)
+            nc.sync.dma_start(out=out_1[rows(t), :], in_=window[:])
+
+        gather_b(0)
+        gather_b(1)
+        scatter_0(0)
+        make_de(1)
+        gather_b(2)
+        make_de(2)
+        make_de(3)
+        scatter_0(1)
+        gather_a(0)
+        gather_a(1)
+        scatter_1(0)
+        scatter_1(1)
+        gather_b(3)
+        gather_a(2)
+        gather_a(3)
+        scatter_0(2)
+        scatter_0(3)
+        scatter_1(2)
+        scatter_1(3)

@@ -20,6 +20,8 @@ PACK = 4
 D_TILES = D // P
 HALF = ITEMS // 2
 WINDOWS = 2
+LIST_STRIPE = 16
+VECTOR_ITEMS = 160
 
 
 def interleave(copy, grouped, raw):
@@ -33,26 +35,29 @@ def tile_attend_gqr_ab_kernel(tc, aT, bT, W, dz, offs, joffs, out_0, out_1):
     nc = tc.nc
     with ExitStack() as ctx:
         keep = ctx.enter_context(tc.tile_pool(name="keep", bufs=1))
+        shared = ctx.enter_context(tc.tile_pool(name="shared", bufs=1))
         psum = ctx.enter_context(tc.psum_pool(name="psum", bufs=1))
 
-        a_list = keep.tile([P, ITEMS // 16], U16, name="a_list")
-        b_list = keep.tile([P, ITEMS // 16], U16, name="b_list")
+        a_list = keep.tile([P, ITEMS // LIST_STRIPE], U16, name="a_list")
+        b_list = keep.tile([P, ITEMS // LIST_STRIPE], U16, name="b_list")
         dz_raw = [keep.tile([P, PACK, HALF], F32, name=f"dz_raw{h}") for h in range(2)]
-        w_first = keep.tile([P, PACK, P], F32, name="w_first")
-        w_rest = keep.tile([P, PACK, D - P], F32, name="w_rest")
+        w_single = [keep.tile([P, PACK, P], F32, name=f"w_single{t}") for t in range(2)]
+        w_rest = keep.tile([P, PACK, 2 * P], F32, name="w_rest")
         a_pair = [keep.tile([P, 2, A_COLS], F32, name=f"a_pair{g}") for g in range(D_TILES // 2)]
         b_tab = [keep.tile([P, B_COLS], F32, name=f"b_tab{t}") for t in range(D_TILES)]
         win_0 = [keep.tile([P, A_COLS], F32, name=f"win_0_{w}") for w in range(WINDOWS)]
-        win_1 = [keep.tile([P, B_COLS], F32, name=f"win_1_{w}") for w in range(WINDOWS)]
+        win_1 = [shared.tile([P, B_COLS], F32, name=f"win_1_{w}", offset=w * 4 * B_COLS) for w in range(WINDOWS)]
         dz_bf = [keep.tile([P, HALF * PACK], BF16, name=f"dz_bf{h}", align_bytes=64) for h in range(2)]
         w_bf = [keep.tile([P, P * PACK], BF16, name=f"w_bf{t}", align_bytes=64) for t in range(D_TILES)]
-        dz_codes = keep.tile([P, ITEMS], U32, name="dz_codes", align_bytes=64)
-        dz_scales = keep.tile([P, ITEMS], U8, name="dz_scales", align_bytes=64)
+        dz_codes = keep.tile([P, HALF + ITEMS], U32, name="dz_codes", align_bytes=64)
+        dz_scales = keep.tile([P, HALF + ITEMS], U8, name="dz_scales", align_bytes=64)
         w_codes = [keep.tile([P, P], U32, name=f"w_codes{t}", align_bytes=64) for t in range(D_TILES)]
         w_scales = [keep.tile([P, P], U8, name=f"w_scales{t}", align_bytes=64) for t in range(D_TILES)]
         de = [keep.tile([P, ITEMS], F32, name=f"de{t}") for t in range(D_TILES)]
         a_got = [keep.tile([P, ITEMS], F32, name=f"a_got{t}") for t in range(D_TILES)]
-        b_got = [keep.tile([P, ITEMS], F32, name=f"b_got{t}") for t in range(D_TILES)]
+        b_got = [shared.tile([P, ITEMS], F32, name="b_got0", offset=4 * B_COLS - 2 * ITEMS)]
+        b_got.extend(keep.tile([P, ITEMS], F32, name=f"b_got{t}") for t in range(1, D_TILES))
+        early_psum = psum.tile([P, ITEMS], F32, name="early_psum")
         de_psum = [psum.tile([P, ITEMS], F32, name=f"de_psum{t}") for t in range(D_TILES)]
 
         dz_rows = dz.rearrange("(p t) i -> p t i", t=PACK)
@@ -61,46 +66,55 @@ def tile_attend_gqr_ab_kernel(tc, aT, bT, W, dz, offs, joffs, out_0, out_1):
         def rows(t):
             return slice(t * P, (t + 1) * P)
 
-        for h in range(2):
-            nc.sync.dma_start(out=dz_raw[h][:], in_=dz_rows[:, :, h * HALF : (h + 1) * HALF])
-        nc.sync.dma_start(out=w_first[:], in_=w_rows[:, :, 0:P])
+        def load_a_pair(g):
+            pair_rows = aT[2 * g * P : 2 * (g + 1) * P, :]
+            nc.sync.dma_start(out=a_pair[g][:], in_=pair_rows.rearrange("(u p) c -> p u c", p=P))
+
+        def load_b(t):
+            nc.sync.dma_start(out=b_tab[t][:], in_=bT[rows(t), :])
+
+        nc.sync.dma_start(out=w_single[0][:], in_=w_rows[:, :, rows(0)])
+        nc.sync.dma_start(out=dz_raw[0][:], in_=dz_rows[:, :, 0:HALF])
         nc.sync.dma_start(b_list[:], joffs)
-        nc.sync.dma_start(out=b_tab[0][:], in_=bT[rows(0), :])
+        load_b(0)
         nc.sync.dma_start(a_list[:], offs)
-        nc.sync.dma_start(out=b_tab[1][:], in_=bT[rows(1), :])
-        nc.sync.dma_start(out=w_rest[:], in_=w_rows[:, :, P:D])
-        nc.sync.dma_start(out=b_tab[2][:], in_=bT[rows(2), :])
-        nc.sync.dma_start(out=a_pair[0][:], in_=aT[0 : 2 * P, :].rearrange("(u p) c -> p u c", p=P))
-        nc.sync.dma_start(out=b_tab[3][:], in_=bT[rows(3), :])
-        nc.sync.dma_start(out=a_pair[1][:], in_=aT[2 * P : 4 * P, :].rearrange("(u p) c -> p u c", p=P))
+        nc.sync.dma_start(out=dz_raw[1][:], in_=dz_rows[:, :, HALF:ITEMS])
+        nc.sync.dma_start(out=w_single[1][:], in_=w_rows[:, :, rows(1)])
+        load_b(1)
+        nc.sync.dma_start(out=w_rest[:], in_=w_rows[:, :, 2 * P : D])
+        load_a_pair(0)
+        load_b(2)
+        load_b(3)
+        load_a_pair(1)
 
-        for w in range(WINDOWS):
-            nc.vector.memset(win_0[w][:].bitcast(I32), 0)
-            nc.vector.memset(win_1[w][:].bitcast(I32), 0)
+        nc.vector.memset(win_0[0][:].bitcast(I32), 0)
+        nc.gpsimd.memset(win_0[1][:].bitcast(I32), 0)
+        nc.vector.memset(dz_codes[:, 0:HALF], 0)
+        nc.vector.memset(dz_scales[:, 0:HALF], 0)
 
-        interleave(nc.scalar.copy, dz_bf[0][:], dz_raw[0][:])
-        interleave(nc.vector.tensor_copy, dz_bf[1][:], dz_raw[1][:])
-        interleave(nc.scalar.copy, w_bf[0][:], w_first[:])
-        for h in range(2):
-            items = slice(h * HALF, (h + 1) * HALF)
-            nc.vector.quantize_mx(out=dz_codes[:, items].bitcast(E5M2X4), scales=dz_scales[:, items], in_=dz_bf[h][:])
+        def quantize_dz(h):
+            cols = slice((h + 1) * HALF, (h + 2) * HALF)
+            nc.vector.quantize_mx(out=dz_codes[:, cols].bitcast(E5M2X4), scales=dz_scales[:, cols], in_=dz_bf[h][:])
 
-        def make_de(t):
+        def quantize_w(t):
             nc.vector.quantize_mx(out=w_codes[t][:].bitcast(E4M3X4), scales=w_scales[t][:], in_=w_bf[t][:])
+
+        def multiply(bank, t, first_col):
+            cols = slice(first_col, first_col + ITEMS)
             nc.tensor.matmul_mx(
-                out=de_psum[t][:],
+                out=bank[:],
                 lhsT=w_codes[t][:].bitcast(E4M3X4),
                 lhsT_scale=w_scales[t][:],
-                rhs=dz_codes[:].bitcast(E5M2X4),
-                rhs_scale=dz_scales[:],
+                rhs=dz_codes[:, cols].bitcast(E5M2X4),
+                rhs_scale=dz_scales[:, cols],
                 start=True,
                 stop=True,
             )
-            nc.scalar.copy(out=de[t][:], in_=de_psum[t][:])
 
-        make_de(0)
-        for t in range(1, D_TILES):
-            interleave(nc.scalar.copy, w_bf[t][:], w_rest[:, :, (t - 1) * P : t * P])
+        def make_de(t):
+            quantize_w(t)
+            multiply(de_psum[t], t, HALF)
+            nc.scalar.copy(out=de[t][:], in_=de_psum[t][:])
 
         def gather_a(t):
             nc.vector.tensor_copy(a_got[t][:], a_pair[t // 2][:, t % 2, :].indirect(a_list[:]))
@@ -108,32 +122,54 @@ def tile_attend_gqr_ab_kernel(tc, aT, bT, W, dz, offs, joffs, out_0, out_1):
         def gather_b(t):
             nc.vector.tensor_copy(b_got[t][:], b_tab[t][:].indirect(b_list[:]))
 
-        def scatter_0(t):
+        def scatter(window, offsets, t, got, first, last):
+            entries = offsets[:, first // LIST_STRIPE : last // LIST_STRIPE]
+            nc.vector.tensor_tensor(window[:].indirect(entries), de[t][:, first:last], got[:, first:last], MULT)
+
+        def put_0(t, first=0):
             window = win_0[t % WINDOWS]
-            nc.vector.tensor_tensor(window[:].indirect(a_list[:]), de[t][:], b_got[t][:], MULT)
+            scatter(window, a_list, t, b_got[t], first, ITEMS)
             nc.sync.dma_start(out=out_0[rows(t), :], in_=window[:])
 
-        def scatter_1(t):
+        def put_1(t):
             window = win_1[t % WINDOWS]
-            nc.vector.tensor_tensor(window[:].indirect(b_list[:]), de[t][:], a_got[t][:], MULT)
+            scatter(window, b_list, t, a_got[t], 0, ITEMS)
             nc.sync.dma_start(out=out_1[rows(t), :], in_=window[:])
 
+        interleave(nc.scalar.copy, w_bf[0][:], w_single[0][:])
+        quantize_w(0)
+        interleave(nc.vector.tensor_copy, dz_bf[0][:, 0 : PACK * VECTOR_ITEMS], dz_raw[0][:, :, 0:VECTOR_ITEMS])
+        interleave(nc.scalar.copy, dz_bf[0][:, PACK * VECTOR_ITEMS :], dz_raw[0][:, :, VECTOR_ITEMS:])
+        quantize_dz(0)
+        multiply(early_psum, 0, 0)
+        nc.scalar.copy(out=de[0][:, 0:HALF], in_=early_psum[:, HALF:ITEMS])
         gather_b(0)
-        gather_b(1)
-        scatter_0(0)
+        scatter(win_0[0], a_list, 0, b_got[0], 0, HALF)
+
+        interleave(nc.scalar.copy, dz_bf[1][:], dz_raw[1][:])
+        interleave(nc.scalar.copy, w_bf[1][:], w_single[1][:])
+        quantize_dz(1)
+        multiply(de_psum[0], 0, HALF)
+        nc.scalar.copy(out=de[0][:, HALF:ITEMS], in_=de_psum[0][:, HALF:ITEMS])
         make_de(1)
-        gather_b(2)
-        make_de(2)
-        make_de(3)
-        scatter_0(1)
-        gather_a(0)
-        gather_a(1)
-        scatter_1(0)
-        scatter_1(1)
-        gather_b(3)
-        gather_a(2)
-        gather_a(3)
-        scatter_0(2)
-        scatter_0(3)
-        scatter_1(2)
-        scatter_1(3)
+        gather_b(1)
+        put_0(0, first=HALF)
+        for w in range(WINDOWS):
+            nc.gpsimd.memset(win_1[w][:].bitcast(I32), 0)
+        put_0(1)
+
+        for t in (2, 3):
+            interleave(nc.scalar.copy, w_bf[t][:], w_rest[:, :, rows(t - 2)])
+            make_de(t)
+        for t in (0, 1):
+            gather_a(t)
+        for t in (0, 1):
+            put_1(t)
+        for t in (2, 3):
+            gather_b(t)
+        for t in (2, 3):
+            gather_a(t)
+        for t in (2, 3):
+            put_0(t)
+        for t in (2, 3):
+            put_1(t)

@@ -87,10 +87,10 @@ def tile_attend_gqr_ab_kernel(tc, aT, bT, W, dz, offs, joffs, out_0, out_1):
         load_b(3)
         load_a_pair(1)
 
-        nc.vector.memset(win_0[0][:].bitcast(I32), 0)
-        nc.gpsimd.memset(win_0[1][:].bitcast(I32), 0)
         nc.vector.memset(dz_codes[:, 0:HALF], 0)
         nc.vector.memset(dz_scales[:, 0:HALF], 0)
+        nc.vector.memset(win_0[0][:].bitcast(I32), 0)
+        nc.vector.memset(win_0[1][:].bitcast(I32), 0)
 
         def quantize_dz(h):
             cols = slice((h + 1) * HALF, (h + 2) * HALF)
@@ -119,8 +119,9 @@ def tile_attend_gqr_ab_kernel(tc, aT, bT, W, dz, offs, joffs, out_0, out_1):
         def gather_a(t):
             nc.vector.tensor_copy(a_got[t][:], a_pair[t // 2][:, t % 2, :].indirect(a_list[:]))
 
-        def gather_b(t):
-            nc.vector.tensor_copy(b_got[t][:], b_tab[t][:].indirect(b_list[:]))
+        def gather_b(t, first=0, last=ITEMS):
+            entries = b_list[:, first // LIST_STRIPE : last // LIST_STRIPE]
+            nc.vector.tensor_copy(b_got[t][:, first:last], b_tab[t][:].indirect(entries))
 
         def scatter(window, offsets, t, got, first, last):
             entries = offsets[:, first // LIST_STRIPE : last // LIST_STRIPE]
@@ -143,7 +144,8 @@ def tile_attend_gqr_ab_kernel(tc, aT, bT, W, dz, offs, joffs, out_0, out_1):
         quantize_dz(0)
         multiply(early_psum, 0, 0)
         nc.scalar.copy(out=de[0][:, 0:HALF], in_=early_psum[:, HALF:ITEMS])
-        gather_b(0)
+        gather_b(0, 0, HALF)
+        gather_b(0, HALF, ITEMS)
         scatter(win_0[0], a_list, 0, b_got[0], 0, HALF)
 
         interleave(nc.scalar.copy, dz_bf[1][:], dz_raw[1][:])

@@ -81,8 +81,8 @@ def tile_attend_gqr_ab_kernel(tc, aT, bT, W, dz, offs, joffs, out_0, out_1):
         nc.sync.dma_start(out=dz_raw[1][:], in_=dz_rows[:, :, HALF:ITEMS])
         nc.sync.dma_start(out=w_single[1][:], in_=w_rows[:, :, rows(1)])
         load_b(1)
-        nc.sync.dma_start(out=w_rest[:], in_=w_rows[:, :, 2 * P : D])
         load_a_pair(0)
+        nc.sync.dma_start(out=w_rest[:], in_=w_rows[:, :, 2 * P : D])
         load_b(2)
         load_b(3)
         load_a_pair(1)
@@ -160,13 +160,13 @@ def tile_attend_gqr_ab_kernel(tc, aT, bT, W, dz, offs, joffs, out_0, out_1):
             nc.gpsimd.memset(win_1[w][:].bitcast(I32), 0)
         put_0(1)
 
+        for t in (0, 1):
+            gather_a(t)
+        put_1(0)
         for t in (2, 3):
             interleave(nc.scalar.copy, w_bf[t][:], w_rest[:, :, rows(t - 2)])
             make_de(t)
-        for t in (0, 1):
-            gather_a(t)
-        for t in (0, 1):
-            put_1(t)
+        put_1(1)
         for t in (2, 3):
             gather_b(t)
         for t in (2, 3):

@@ -40,7 +40,10 @@ def tile_attend_gqr_ab_kernel(tc, aT, bT, W, dz, offs, joffs, out_0, out_1):
 
         a_list = keep.tile([P, ITEMS // LIST_STRIPE], U16, name="a_list")
         b_list = keep.tile([P, ITEMS // LIST_STRIPE], U16, name="b_list")
-        dz_raw = [keep.tile([P, PACK, HALF], F32, name=f"dz_raw{h}") for h in range(2)]
+        dz_raw = [
+            keep.tile([P, PACK, HALF], F32, name="dz_raw0"),
+            shared.tile([P, PACK, HALF], F32, name="dz_raw1", offset=WINDOWS * 4 * B_COLS),
+        ]
         w_single = [keep.tile([P, PACK, P], F32, name=f"w_single{t}") for t in range(2)]
         w_rest = keep.tile([P, PACK, 2 * P], F32, name="w_rest")
         a_pair = [keep.tile([P, 2, A_COLS], F32, name=f"a_pair{g}") for g in range(D_TILES // 2)]
@@ -56,7 +59,9 @@ def tile_attend_gqr_ab_kernel(tc, aT, bT, W, dz, offs, joffs, out_0, out_1):
         de = [keep.tile([P, ITEMS], F32, name=f"de{t}") for t in range(D_TILES)]
         a_got = [keep.tile([P, ITEMS], F32, name=f"a_got{t}") for t in range(D_TILES)]
         b_got = [shared.tile([P, ITEMS], F32, name="b_got0", offset=4 * B_COLS - 2 * ITEMS)]
-        b_got.extend(keep.tile([P, ITEMS], F32, name=f"b_got{t}") for t in range(1, D_TILES))
+        b_got.append(keep.tile([P, ITEMS], F32, name="b_got1"))
+        b_got.append(shared.tile([P, ITEMS], F32, name="b_got2", offset=WINDOWS * 4 * B_COLS))
+        b_got.append(keep.tile([P, ITEMS], F32, name="b_got3"))
         early_psum = psum.tile([P, ITEMS], F32, name="early_psum")
         de_psum = [psum.tile([P, ITEMS], F32, name=f"de_psum{t}") for t in range(D_TILES)]
 
@@ -78,13 +83,13 @@ def tile_attend_gqr_ab_kernel(tc, aT, bT, W, dz, offs, joffs, out_0, out_1):
         nc.sync.dma_start(b_list[:], joffs)
         load_b(0)
         nc.sync.dma_start(a_list[:], offs)
-        nc.sync.dma_start(out=dz_raw[1][:], in_=dz_rows[:, :, HALF:ITEMS])
-        nc.sync.dma_start(out=w_single[1][:], in_=w_rows[:, :, rows(1)])
         load_b(1)
+        nc.sync.dma_start(out=dz_raw[1][:], in_=dz_rows[:, :, HALF:ITEMS])
+        load_b(2)
+        nc.sync.dma_start(out=w_single[1][:], in_=w_rows[:, :, rows(1)])
+        load_b(3)
         load_a_pair(0)
         nc.sync.dma_start(out=w_rest[:], in_=w_rows[:, :, 2 * P : D])
-        load_b(2)
-        load_b(3)
         load_a_pair(1)
 
         nc.vector.memset(dz_codes[:, 0:HALF], 0)
@@ -144,8 +149,8 @@ def tile_attend_gqr_ab_kernel(tc, aT, bT, W, dz, offs, joffs, out_0, out_1):
         quantize_dz(0)
         multiply(early_psum, 0, 0)
         nc.scalar.copy(out=de[0][:, 0:HALF], in_=early_psum[:, HALF:ITEMS])
-        gather_b(0, 0, HALF)
-        gather_b(0, HALF, ITEMS)
+        gather_b(0)
+        gather_b(1)
         scatter(win_0[0], a_list, 0, b_got[0], 0, HALF)
 
         interleave(nc.scalar.copy, dz_bf[1][:], dz_raw[1][:])
@@ -153,8 +158,9 @@ def tile_attend_gqr_ab_kernel(tc, aT, bT, W, dz, offs, joffs, out_0, out_1):
         quantize_dz(1)
         multiply(de_psum[0], 0, HALF)
         nc.scalar.copy(out=de[0][:, HALF:ITEMS], in_=de_psum[0][:, HALF:ITEMS])
+        gather_b(2)
         make_de(1)
-        gather_b(1)
+        gather_b(3)
         put_0(0, first=HALF)
         for w in range(WINDOWS):
             nc.gpsimd.memset(win_1[w][:].bitcast(I32), 0)
@@ -167,8 +173,6 @@ def tile_attend_gqr_ab_kernel(tc, aT, bT, W, dz, offs, joffs, out_0, out_1):
             interleave(nc.scalar.copy, w_bf[t][:], w_rest[:, :, rows(t - 2)])
             make_de(t)
         put_1(1)
-        for t in (2, 3):
-            gather_b(t)
         for t in (2, 3):
             gather_a(t)
         for t in (2, 3):

@@ -41,7 +41,7 @@ def tile_attend_gqr_ab_kernel(tc, aT, bT, W, dz, offs, joffs, out_0, out_1):
         a_list = keep.tile([P, ITEMS // LIST_STRIPE], U16, name="a_list")
         b_list = keep.tile([P, ITEMS // LIST_STRIPE], U16, name="b_list")
         dz_raw = [
-            keep.tile([P, PACK, HALF], F32, name="dz_raw0"),
+            shared.tile([P, PACK, HALF], F32, name="dz_raw0", offset=WINDOWS * 4 * B_COLS + 4 * PACK * HALF),
             shared.tile([P, PACK, HALF], F32, name="dz_raw1", offset=WINDOWS * 4 * B_COLS),
         ]
         w_single = [keep.tile([P, PACK, P], F32, name=f"w_single{t}") for t in range(2)]
@@ -58,7 +58,7 @@ def tile_attend_gqr_ab_kernel(tc, aT, bT, W, dz, offs, joffs, out_0, out_1):
         w_scales = [keep.tile([P, P], U8, name=f"w_scales{t}", align_bytes=64) for t in range(D_TILES)]
         de = [keep.tile([P, ITEMS], F32, name=f"de{t}") for t in range(D_TILES)]
         a_got = [keep.tile([P, ITEMS], F32, name=f"a_got{t}") for t in range(D_TILES)]
-        b_got = [shared.tile([P, ITEMS], F32, name="b_got0", offset=4 * B_COLS - 2 * ITEMS)]
+        b_got = [shared.tile([P, ITEMS], F32, name="b_got0", offset=WINDOWS * 4 * B_COLS + 4 * PACK * HALF)]
         b_got.append(keep.tile([P, ITEMS], F32, name="b_got1"))
         b_got.append(shared.tile([P, ITEMS], F32, name="b_got2", offset=WINDOWS * 4 * B_COLS))
         b_got.append(keep.tile([P, ITEMS], F32, name="b_got3"))
@@ -96,6 +96,8 @@ def tile_attend_gqr_ab_kernel(tc, aT, bT, W, dz, offs, joffs, out_0, out_1):
         nc.vector.memset(dz_scales[:, 0:HALF], 0)
         nc.vector.memset(win_0[0][:].bitcast(I32), 0)
         nc.vector.memset(win_0[1][:].bitcast(I32), 0)
+        for w in range(WINDOWS):
+            nc.vector.memset(win_1[w][:].bitcast(I32), 0)
 
         def quantize_dz(h):
             cols = slice((h + 1) * HALF, (h + 2) * HALF)
@@ -162,8 +164,6 @@ def tile_attend_gqr_ab_kernel(tc, aT, bT, W, dz, offs, joffs, out_0, out_1):
         make_de(1)
         gather_b(3)
         put_0(0, first=HALF)
-        for w in range(WINDOWS):
-            nc.gpsimd.memset(win_1[w][:].bitcast(I32), 0)
         put_0(1)
 
         for t in (0, 1):

@@ -44,9 +44,10 @@ def tile_attend_gqr_ab_kernel(tc, aT, bT, W, dz, offs, joffs, out_0, out_1):
             shared.tile([P, PACK, HALF], F32, name="dz_raw0", offset=WINDOWS * 4 * B_COLS + 4 * PACK * HALF),
             shared.tile([P, PACK, HALF], F32, name="dz_raw1", offset=WINDOWS * 4 * B_COLS),
         ]
-        w_single = [keep.tile([P, PACK, P], F32, name=f"w_single{t}") for t in range(2)]
-        w_rest = keep.tile([P, PACK, 2 * P], F32, name="w_rest")
-        a_pair = [keep.tile([P, 2, A_COLS], F32, name=f"a_pair{g}") for g in range(D_TILES // 2)]
+        w_single = [keep.tile([P, PACK, P], F32, name=f"w_single{t}") for t in range(D_TILES)]
+        a_pair = keep.tile([P, 2, A_COLS], F32, name="a_pair")
+        a_late = [shared.tile([P, A_COLS], F32, name=f"a_late{t}", offset=(12 + 8 * t) * 1024) for t in range(2)]
+        a_tab = [a_pair[:, 0, :], a_pair[:, 1, :], a_late[0][:], a_late[1][:]]
         b_tab = [keep.tile([P, B_COLS], F32, name=f"b_tab{t}") for t in range(D_TILES)]
         win_0 = [keep.tile([P, A_COLS], F32, name=f"win_0_{w}") for w in range(WINDOWS)]
         win_1 = [shared.tile([P, B_COLS], F32, name=f"win_1_{w}", offset=w * 4 * B_COLS) for w in range(WINDOWS)]
@@ -59,7 +60,7 @@ def tile_attend_gqr_ab_kernel(tc, aT, bT, W, dz, offs, joffs, out_0, out_1):
         de = [keep.tile([P, ITEMS], F32, name=f"de{t}") for t in range(D_TILES)]
         a_got = [keep.tile([P, ITEMS], F32, name=f"a_got{t}") for t in range(D_TILES)]
         b_got = [shared.tile([P, ITEMS], F32, name="b_got0", offset=WINDOWS * 4 * B_COLS + 4 * PACK * HALF)]
-        b_got.append(keep.tile([P, ITEMS], F32, name="b_got1"))
+        b_got.append(shared.tile([P, ITEMS], F32, name="b_got1", offset=20 * 1024))
         b_got.append(shared.tile([P, ITEMS], F32, name="b_got2", offset=WINDOWS * 4 * B_COLS))
         b_got.append(keep.tile([P, ITEMS], F32, name="b_got3"))
         early_psum = psum.tile([P, ITEMS], F32, name="early_psum")
@@ -71,9 +72,8 @@ def tile_attend_gqr_ab_kernel(tc, aT, bT, W, dz, offs, joffs, out_0, out_1):
         def rows(t):
             return slice(t * P, (t + 1) * P)
 
-        def load_a_pair(g):
-            pair_rows = aT[2 * g * P : 2 * (g + 1) * P, :]
-            nc.sync.dma_start(out=a_pair[g][:], in_=pair_rows.rearrange("(u p) c -> p u c", p=P))
+        def load_a(t):
+            nc.sync.dma_start(out=a_tab[t], in_=aT[rows(t), :])
 
         def load_b(t):
             nc.sync.dma_start(out=b_tab[t][:], in_=bT[rows(t), :])
@@ -88,9 +88,9 @@ def tile_attend_gqr_ab_kernel(tc, aT, bT, W, dz, offs, joffs, out_0, out_1):
         load_b(2)
         nc.sync.dma_start(out=w_single[1][:], in_=w_rows[:, :, rows(1)])
         load_b(3)
-        load_a_pair(0)
-        nc.sync.dma_start(out=w_rest[:], in_=w_rows[:, :, 2 * P : D])
-        load_a_pair(1)
+        nc.sync.dma_start(out=w_single[2][:], in_=w_rows[:, :, rows(2)])
+        nc.sync.dma_start(out=a_pair[:], in_=aT[0 : 2 * P, :].rearrange("(u p) c -> p u c", p=P))
+        nc.sync.dma_start(out=w_single[3][:], in_=w_rows[:, :, rows(3)])
 
         nc.vector.memset(dz_codes[:, 0:HALF], 0)
         nc.vector.memset(dz_scales[:, 0:HALF], 0)
@@ -123,8 +123,9 @@ def tile_attend_gqr_ab_kernel(tc, aT, bT, W, dz, offs, joffs, out_0, out_1):
             multiply(de_psum[t], t, HALF)
             nc.scalar.copy(out=de[t][:], in_=de_psum[t][:])
 
-        def gather_a(t):
-            nc.vector.tensor_copy(a_got[t][:], a_pair[t // 2][:, t % 2, :].indirect(a_list[:]))
+        def gather_a(t, first=0, last=ITEMS):
+            entries = a_list[:, first // LIST_STRIPE : last // LIST_STRIPE]
+            nc.vector.tensor_copy(a_got[t][:, first:last], a_tab[t].indirect(entries))
 
         def gather_b(t, first=0, last=ITEMS):
             entries = b_list[:, first // LIST_STRIPE : last // LIST_STRIPE]
@@ -139,9 +140,9 @@ def tile_attend_gqr_ab_kernel(tc, aT, bT, W, dz, offs, joffs, out_0, out_1):
             scatter(window, a_list, t, b_got[t], first, ITEMS)
             nc.sync.dma_start(out=out_0[rows(t), :], in_=window[:])
 
-        def put_1(t):
+        def put_1(t, first=0):
             window = win_1[t % WINDOWS]
-            scatter(window, b_list, t, a_got[t], 0, ITEMS)
+            scatter(window, b_list, t, a_got[t], first, ITEMS)
             nc.sync.dma_start(out=out_1[rows(t), :], in_=window[:])
 
         interleave(nc.scalar.copy, w_bf[0][:], w_single[0][:])
@@ -164,18 +165,23 @@ def tile_attend_gqr_ab_kernel(tc, aT, bT, W, dz, offs, joffs, out_0, out_1):
         make_de(1)
         gather_b(3)
         put_0(0, first=HALF)
+        load_a(2)
         put_0(1)
+        load_a(3)
 
+        interleave(nc.scalar.copy, w_bf[2][:], w_single[2][:])
+        make_de(2)
         for t in (0, 1):
-            gather_a(t)
-        put_1(0)
-        for t in (2, 3):
-            interleave(nc.scalar.copy, w_bf[t][:], w_rest[:, :, rows(t - 2)])
-            make_de(t)
-        put_1(1)
-        for t in (2, 3):
-            gather_a(t)
+            gather_a(t, 0, HALF)
+        for t in (0, 1):
+            scatter(win_1[t], b_list, t, a_got[t], 0, HALF)
+            gather_a(t, HALF, ITEMS)
+        for t in (0, 1):
+            put_1(t, first=HALF)
+        interleave(nc.scalar.copy, w_bf[3][:], w_single[3][:])
+        make_de(3)
         for t in (2, 3):
             put_0(t)
+            gather_a(t)
         for t in (2, 3):
             put_1(t)

@@ -22,6 +22,9 @@ HALF = ITEMS // 2
 WINDOWS = 2
 LIST_STRIPE = 16
 VECTOR_ITEMS = 160
+HELD = 16
+RAW_W = PACK * P
+KIB = 1024
 
 
 def interleave(copy, grouped, raw):
@@ -40,29 +43,38 @@ def tile_attend_gqr_ab_kernel(tc, aT, bT, W, dz, offs, joffs, out_0, out_1):
 
         a_list = keep.tile([P, ITEMS // LIST_STRIPE], U16, name="a_list")
         b_list = keep.tile([P, ITEMS // LIST_STRIPE], U16, name="b_list")
+
         dz_raw = [
-            shared.tile([P, PACK, HALF], F32, name="dz_raw0", offset=WINDOWS * 4 * B_COLS + 4 * PACK * HALF),
-            shared.tile([P, PACK, HALF], F32, name="dz_raw1", offset=WINDOWS * 4 * B_COLS),
+            shared.tile([P, PACK, HALF], F32, name="dz_raw0", offset=10 * KIB),
+            shared.tile([P, PACK, HALF], F32, name="dz_raw1", offset=0),
         ]
-        w_single = [keep.tile([P, PACK, P], F32, name=f"w_single{t}") for t in range(D_TILES)]
-        a_pair = keep.tile([P, 2, A_COLS], F32, name="a_pair")
-        a_late = [shared.tile([P, A_COLS], F32, name=f"a_late{t}", offset=(12 + 8 * t) * 1024) for t in range(2)]
-        a_tab = [a_pair[:, 0, :], a_pair[:, 1, :], a_late[0][:], a_late[1][:]]
+        with_w2 = keep.tile([P, RAW_W + ITEMS - HELD], F32, name="with_w2")
+        with_w3_cols = RAW_W + 2 * (ITEMS - HELD)
+        with_w3 = shared.tile([P, with_w3_cols], F32, name="with_w3", offset=12 * KIB - 4 * with_w3_cols)
+        w_raw = [keep.tile([P, PACK, P], F32, name=f"w_raw{t}") for t in range(2)]
+        w_raw.append(with_w2[:, 0:RAW_W].rearrange("p (t d) -> p t d", t=PACK))
+        w_raw.append(with_w3[:, ITEMS - HELD : ITEMS - HELD + RAW_W].rearrange("p (t d) -> p t d", t=PACK))
+        a_tab = [keep.tile([P, A_COLS], F32, name="a_tab0")]
+        a_tab = a_tab + [shared.tile([P, A_COLS], F32, name=f"a_tab{t}", offset=(4 + 8 * t) * KIB) for t in (1, 2, 3)]
         b_tab = [keep.tile([P, B_COLS], F32, name=f"b_tab{t}") for t in range(D_TILES)]
         win_0 = [keep.tile([P, A_COLS], F32, name=f"win_0_{w}") for w in range(WINDOWS)]
-        win_1 = [shared.tile([P, B_COLS], F32, name=f"win_1_{w}", offset=w * 4 * B_COLS) for w in range(WINDOWS)]
+        win_1 = [keep.tile([P, B_COLS], F32, name=f"win_1_{w}") for w in range(WINDOWS)]
         dz_bf = [keep.tile([P, HALF * PACK], BF16, name=f"dz_bf{h}", align_bytes=64) for h in range(2)]
         w_bf = [keep.tile([P, P * PACK], BF16, name=f"w_bf{t}", align_bytes=64) for t in range(D_TILES)]
         dz_codes = keep.tile([P, HALF + ITEMS], U32, name="dz_codes", align_bytes=64)
         dz_scales = keep.tile([P, HALF + ITEMS], U8, name="dz_scales", align_bytes=64)
         w_codes = [keep.tile([P, P], U32, name=f"w_codes{t}", align_bytes=64) for t in range(D_TILES)]
         w_scales = [keep.tile([P, P], U8, name=f"w_scales{t}", align_bytes=64) for t in range(D_TILES)]
-        de = [keep.tile([P, ITEMS], F32, name=f"de{t}") for t in range(D_TILES)]
+        de = [shared.tile([P, ITEMS], F32, name="de0", offset=20 * KIB), with_w2[:, RAW_W - HELD :]]
+        de = de + [keep.tile([P, ITEMS], F32, name=f"de{t}") for t in (2, 3)]
+        de_late = [with_w3[:, 0:ITEMS], with_w3[:, with_w3_cols - ITEMS :], de[2], de[3]]
         a_got = [keep.tile([P, ITEMS], F32, name=f"a_got{t}") for t in range(D_TILES)]
-        b_got = [shared.tile([P, ITEMS], F32, name="b_got0", offset=WINDOWS * 4 * B_COLS + 4 * PACK * HALF)]
-        b_got.append(shared.tile([P, ITEMS], F32, name="b_got1", offset=20 * 1024))
-        b_got.append(shared.tile([P, ITEMS], F32, name="b_got2", offset=WINDOWS * 4 * B_COLS))
-        b_got.append(keep.tile([P, ITEMS], F32, name="b_got3"))
+        b_got = [
+            shared.tile([P, ITEMS], F32, name="b_got0", offset=11 * KIB),
+            shared.tile([P, ITEMS], F32, name="b_got1", offset=28 * KIB),
+            shared.tile([P, ITEMS], F32, name="b_got2", offset=0),
+            keep.tile([P, ITEMS], F32, name="b_got3"),
+        ]
         early_psum = psum.tile([P, ITEMS], F32, name="early_psum")
         de_psum = [psum.tile([P, ITEMS], F32, name=f"de_psum{t}") for t in range(D_TILES)]
 
@@ -73,31 +85,19 @@ def tile_attend_gqr_ab_kernel(tc, aT, bT, W, dz, offs, joffs, out_0, out_1):
             return slice(t * P, (t + 1) * P)
 
         def load_a(t):
-            nc.sync.dma_start(out=a_tab[t], in_=aT[rows(t), :])
+            nc.sync.dma_start(out=a_tab[t][:], in_=aT[rows(t), :])
 
         def load_b(t):
             nc.sync.dma_start(out=b_tab[t][:], in_=bT[rows(t), :])
 
-        nc.sync.dma_start(out=w_single[0][:], in_=w_rows[:, :, rows(0)])
-        nc.sync.dma_start(out=dz_raw[0][:], in_=dz_rows[:, :, 0:HALF])
-        nc.sync.dma_start(b_list[:], joffs)
-        load_b(0)
-        nc.sync.dma_start(a_list[:], offs)
-        load_b(1)
-        nc.sync.dma_start(out=dz_raw[1][:], in_=dz_rows[:, :, HALF:ITEMS])
-        load_b(2)
-        nc.sync.dma_start(out=w_single[1][:], in_=w_rows[:, :, rows(1)])
-        load_b(3)
-        nc.sync.dma_start(out=w_single[2][:], in_=w_rows[:, :, rows(2)])
-        nc.sync.dma_start(out=a_pair[:], in_=aT[0 : 2 * P, :].rearrange("(u p) c -> p u c", p=P))
-        nc.sync.dma_start(out=w_single[3][:], in_=w_rows[:, :, rows(3)])
+        def load_w(t):
+            nc.sync.dma_start(out=w_raw[t][:], in_=w_rows[:, :, rows(t)])
 
-        nc.vector.memset(dz_codes[:, 0:HALF], 0)
-        nc.vector.memset(dz_scales[:, 0:HALF], 0)
-        nc.vector.memset(win_0[0][:].bitcast(I32), 0)
-        nc.vector.memset(win_0[1][:].bitcast(I32), 0)
-        for w in range(WINDOWS):
-            nc.vector.memset(win_1[w][:].bitcast(I32), 0)
+        def load_dz(h):
+            nc.sync.dma_start(out=dz_raw[h][:], in_=dz_rows[:, :, h * HALF : (h + 1) * HALF])
+
+        def cast_w(t):
+            interleave(nc.scalar.copy, w_bf[t][:], w_raw[t][:])
 
         def quantize_dz(h):
             cols = slice((h + 1) * HALF, (h + 2) * HALF)
@@ -118,34 +118,53 @@ def tile_attend_gqr_ab_kernel(tc, aT, bT, W, dz, offs, joffs, out_0, out_1):
                 stop=True,
             )
 
+        def copy_de(target, t, first, last):
+            nc.scalar.copy(out=target[t][:, first:last], in_=de_psum[t][:, first:last])
+
         def make_de(t):
             quantize_w(t)
             multiply(de_psum[t], t, HALF)
-            nc.scalar.copy(out=de[t][:], in_=de_psum[t][:])
+            copy_de(de, t, 0, ITEMS)
 
-        def gather_a(t, first=0, last=ITEMS):
+        def gather_a(t):
+            nc.vector.tensor_copy(a_got[t][:], a_tab[t][:].indirect(a_list[:]))
+
+        def gather_b(t):
+            nc.vector.tensor_copy(b_got[t][:], b_tab[t][:].indirect(b_list[:]))
+
+        def scatter_0(t, first, last):
             entries = a_list[:, first // LIST_STRIPE : last // LIST_STRIPE]
-            nc.vector.tensor_copy(a_got[t][:, first:last], a_tab[t].indirect(entries))
-
-        def gather_b(t, first=0, last=ITEMS):
-            entries = b_list[:, first // LIST_STRIPE : last // LIST_STRIPE]
-            nc.vector.tensor_copy(b_got[t][:, first:last], b_tab[t][:].indirect(entries))
-
-        def scatter(window, offsets, t, got, first, last):
-            entries = offsets[:, first // LIST_STRIPE : last // LIST_STRIPE]
-            nc.vector.tensor_tensor(window[:].indirect(entries), de[t][:, first:last], got[:, first:last], MULT)
+            window = win_0[t % WINDOWS][:].indirect(entries)
+            nc.vector.tensor_tensor(window, de[t][:, first:last], b_got[t][:, first:last], MULT)
 
         def put_0(t, first=0):
-            window = win_0[t % WINDOWS]
-            scatter(window, a_list, t, b_got[t], first, ITEMS)
-            nc.sync.dma_start(out=out_0[rows(t), :], in_=window[:])
+            scatter_0(t, first, ITEMS)
+            nc.sync.dma_start(out=out_0[rows(t), :], in_=win_0[t % WINDOWS][:])
 
-        def put_1(t, first=0):
+        def put_1(t):
             window = win_1[t % WINDOWS]
-            scatter(window, b_list, t, a_got[t], first, ITEMS)
+            nc.vector.tensor_tensor(window[:].indirect(b_list[:]), de_late[t][:], a_got[t][:], MULT)
             nc.sync.dma_start(out=out_1[rows(t), :], in_=window[:])
 
-        interleave(nc.scalar.copy, w_bf[0][:], w_single[0][:])
+        load_w(0)
+        load_dz(0)
+        nc.sync.dma_start(b_list[:], joffs)
+        load_b(0)
+        nc.sync.dma_start(a_list[:], offs)
+        load_b(1)
+        load_dz(1)
+        load_b(2)
+        load_w(1)
+        load_b(3)
+        load_w(2)
+        load_a(0)
+
+        nc.vector.memset(dz_codes[:, 0:HALF], 0)
+        nc.vector.memset(dz_scales[:, 0:HALF], 0)
+        for window in win_0 + win_1:
+            nc.vector.memset(window[:].bitcast(I32), 0)
+
+        cast_w(0)
         quantize_w(0)
         interleave(nc.vector.tensor_copy, dz_bf[0][:, 0 : PACK * VECTOR_ITEMS], dz_raw[0][:, :, 0:VECTOR_ITEMS])
         interleave(nc.scalar.copy, dz_bf[0][:, PACK * VECTOR_ITEMS :], dz_raw[0][:, :, VECTOR_ITEMS:])
@@ -154,34 +173,42 @@ def tile_attend_gqr_ab_kernel(tc, aT, bT, W, dz, offs, joffs, out_0, out_1):
         nc.scalar.copy(out=de[0][:, 0:HALF], in_=early_psum[:, HALF:ITEMS])
         gather_b(0)
         gather_b(1)
-        scatter(win_0[0], a_list, 0, b_got[0], 0, HALF)
+        scatter_0(0, 0, HALF)
 
         interleave(nc.scalar.copy, dz_bf[1][:], dz_raw[1][:])
-        interleave(nc.scalar.copy, w_bf[1][:], w_single[1][:])
+        cast_w(1)
         quantize_dz(1)
         multiply(de_psum[0], 0, HALF)
-        nc.scalar.copy(out=de[0][:, HALF:ITEMS], in_=de_psum[0][:, HALF:ITEMS])
+        copy_de(de, 0, HALF, ITEMS)
         gather_b(2)
-        make_de(1)
+        quantize_w(1)
+        multiply(de_psum[1], 1, HALF)
+        copy_de(de, 1, HELD, ITEMS)
         gather_b(3)
         put_0(0, first=HALF)
+        load_a(1)
+        load_w(3)
         load_a(2)
+
+        cast_w(2)
+        copy_de(de, 1, 0, HELD)
+        make_de(2)
         put_0(1)
         load_a(3)
+        copy_de(de_late, 0, 0, ITEMS - HELD)
+        copy_de(de_late, 1, HELD, ITEMS)
+        gather_a(0)
+        put_0(2)
+        gather_a(1)
 
-        interleave(nc.scalar.copy, w_bf[2][:], w_single[2][:])
-        make_de(2)
-        for t in (0, 1):
-            gather_a(t, 0, HALF)
-        for t in (0, 1):
-            scatter(win_1[t], b_list, t, a_got[t], 0, HALF)
-            gather_a(t, HALF, ITEMS)
-        for t in (0, 1):
-            put_1(t, first=HALF)
-        interleave(nc.scalar.copy, w_bf[3][:], w_single[3][:])
+        cast_w(3)
+        copy_de(de_late, 0, ITEMS - HELD, ITEMS)
+        copy_de(de_late, 1, 0, HELD)
         make_de(3)
-        for t in (2, 3):
-            put_0(t)
-            gather_a(t)
-        for t in (2, 3):
-            put_1(t)
+        put_1(0)
+        put_1(1)
+        gather_a(2)
+        put_0(3)
+        gather_a(3)
+        put_1(2)
+        put_1(3)

@@ -14,16 +14,14 @@ U8 = mybir.dt.uint8
 E4M3X4 = mybir.dt.float8_e4m3fn_x4
 E5M2X4 = mybir.dt.float8_e5m2_x4
 MULT = mybir.AluOpType.mult
+COPY = mybir.ActivationFunctionType.Copy
 
 P = 128
 PACK = 4
 D_TILES = D // P
 HALF = ITEMS // 2
-WINDOWS = 2
+PAIR = 2 * P
 LIST_STRIPE = 16
-VECTOR_ITEMS = 160
-HELD = 16
-RAW_W = PACK * P
 KIB = 1024
 
 
@@ -43,39 +41,29 @@ def tile_attend_gqr_ab_kernel(tc, aT, bT, W, dz, offs, joffs, out_0, out_1):
 
         a_list = keep.tile([P, ITEMS // LIST_STRIPE], U16, name="a_list")
         b_list = keep.tile([P, ITEMS // LIST_STRIPE], U16, name="b_list")
-
-        dz_raw = [
-            shared.tile([P, PACK, HALF], F32, name="dz_raw0", offset=10 * KIB),
-            shared.tile([P, PACK, HALF], F32, name="dz_raw1", offset=0),
-        ]
-        with_w2 = keep.tile([P, RAW_W + ITEMS - HELD], F32, name="with_w2")
-        with_w3_cols = RAW_W + 2 * (ITEMS - HELD)
-        with_w3 = shared.tile([P, with_w3_cols], F32, name="with_w3", offset=12 * KIB - 4 * with_w3_cols)
-        w_raw = [keep.tile([P, PACK, P], F32, name=f"w_raw{t}") for t in range(2)]
-        w_raw.append(with_w2[:, 0:RAW_W].rearrange("p (t d) -> p t d", t=PACK))
-        w_raw.append(with_w3[:, ITEMS - HELD : ITEMS - HELD + RAW_W].rearrange("p (t d) -> p t d", t=PACK))
-        a_tab = [keep.tile([P, A_COLS], F32, name="a_tab0")]
-        a_tab = a_tab + [shared.tile([P, A_COLS], F32, name=f"a_tab{t}", offset=(4 + 8 * t) * KIB) for t in (1, 2, 3)]
+        dz_raw = [keep.tile([P, PACK, HALF], F32, name=f"dz_raw{h}") for h in range(2)]
+        w_raw = [keep.tile([P, PACK, PAIR], F32, name=f"w_raw{h}") for h in range(2)]
+        a_tab = [keep.tile([P, A_COLS], F32, name=f"a_tab{t}") for t in range(D_TILES)]
         b_tab = [keep.tile([P, B_COLS], F32, name=f"b_tab{t}") for t in range(D_TILES)]
-        win_0 = [keep.tile([P, A_COLS], F32, name=f"win_0_{w}") for w in range(WINDOWS)]
-        win_1 = [keep.tile([P, B_COLS], F32, name=f"win_1_{w}") for w in range(WINDOWS)]
-        dz_bf = [keep.tile([P, HALF * PACK], BF16, name=f"dz_bf{h}", align_bytes=64) for h in range(2)]
-        w_bf = [keep.tile([P, P * PACK], BF16, name=f"w_bf{t}", align_bytes=64) for t in range(D_TILES)]
-        dz_codes = keep.tile([P, HALF + ITEMS], U32, name="dz_codes", align_bytes=64)
-        dz_scales = keep.tile([P, HALF + ITEMS], U8, name="dz_scales", align_bytes=64)
-        w_codes = [keep.tile([P, P], U32, name=f"w_codes{t}", align_bytes=64) for t in range(D_TILES)]
-        w_scales = [keep.tile([P, P], U8, name=f"w_scales{t}", align_bytes=64) for t in range(D_TILES)]
-        de = [shared.tile([P, ITEMS], F32, name="de0", offset=20 * KIB), with_w2[:, RAW_W - HELD :]]
-        de = de + [keep.tile([P, ITEMS], F32, name=f"de{t}") for t in (2, 3)]
-        de_late = [with_w3[:, 0:ITEMS], with_w3[:, with_w3_cols - ITEMS :], de[2], de[3]]
-        a_got = [keep.tile([P, ITEMS], F32, name=f"a_got{t}") for t in range(D_TILES)]
-        b_got = [
-            shared.tile([P, ITEMS], F32, name="b_got0", offset=11 * KIB),
-            shared.tile([P, ITEMS], F32, name="b_got1", offset=28 * KIB),
-            shared.tile([P, ITEMS], F32, name="b_got2", offset=0),
-            keep.tile([P, ITEMS], F32, name="b_got3"),
+        win_0 = [keep.tile([P, A_COLS], F32, name=f"win_0_{t}") for t in range(D_TILES)]
+        win_1 = [shared.tile([P, B_COLS], F32, name=f"win_1_{t}", offset=4 * t * KIB) for t in range(D_TILES)]
+        dz_bf = [
+            keep.tile([P, HALF * PACK], BF16, name="dz_bf0", align_bytes=64),
+            shared.tile([P, HALF * PACK], BF16, name="dz_bf1", align_bytes=64, offset=3 * KIB),
         ]
-        early_psum = psum.tile([P, ITEMS], F32, name="early_psum")
+        w_bf = [
+            keep.tile([P, PAIR * PACK], BF16, name="w_bf0", align_bytes=64),
+            shared.tile([P, PAIR * PACK], BF16, name="w_bf1", align_bytes=64, offset=11 * KIB),
+        ]
+        dz_codes = keep.tile([P, ITEMS], U32, name="dz_codes", align_bytes=64)
+        dz_scales = keep.tile([P, ITEMS], U8, name="dz_scales", align_bytes=64)
+        w_codes = [keep.tile([P, PAIR], U32, name=f"w_codes{h}", align_bytes=64) for h in range(2)]
+        w_scales = [keep.tile([P, PAIR], U8, name=f"w_scales{h}", align_bytes=64) for h in range(2)]
+        de = {t: keep.tile([P, ITEMS], F32, name=f"de{t}") for t in (0, 2)}
+        da = {t: keep.tile([P, ITEMS], F32, name=f"da{t}") for t in (1, 3)}
+        db = {t: keep.tile([P, ITEMS], F32, name=f"db{t}") for t in (1, 3)}
+        a_got = [keep.tile([P, ITEMS], F32, name=f"a_got{t}") for t in range(D_TILES)]
+        b_got = [keep.tile([P, ITEMS], F32, name=f"b_got{t}") for t in range(D_TILES)]
         de_psum = [psum.tile([P, ITEMS], F32, name=f"de_psum{t}") for t in range(D_TILES)]
 
         dz_rows = dz.rearrange("(p t) i -> p t i", t=PACK)
@@ -90,125 +78,108 @@ def tile_attend_gqr_ab_kernel(tc, aT, bT, W, dz, offs, joffs, out_0, out_1):
         def load_b(t):
             nc.sync.dma_start(out=b_tab[t][:], in_=bT[rows(t), :])
 
-        def load_w(t):
-            nc.sync.dma_start(out=w_raw[t][:], in_=w_rows[:, :, rows(t)])
+        def load_w(h):
+            nc.sync.dma_start(out=w_raw[h][:], in_=w_rows[:, :, h * PAIR : (h + 1) * PAIR])
 
         def load_dz(h):
             nc.sync.dma_start(out=dz_raw[h][:], in_=dz_rows[:, :, h * HALF : (h + 1) * HALF])
 
-        def cast_w(t):
-            interleave(nc.scalar.copy, w_bf[t][:], w_raw[t][:])
+        def cast(copy, grouped, raw, first, last):
+            interleave(copy, grouped[:, PACK * first : PACK * last], raw[:, :, first:last])
 
         def quantize_dz(h):
-            cols = slice((h + 1) * HALF, (h + 2) * HALF)
+            cols = slice(h * HALF, (h + 1) * HALF)
             nc.vector.quantize_mx(out=dz_codes[:, cols].bitcast(E5M2X4), scales=dz_scales[:, cols], in_=dz_bf[h][:])
 
-        def quantize_w(t):
-            nc.vector.quantize_mx(out=w_codes[t][:].bitcast(E4M3X4), scales=w_scales[t][:], in_=w_bf[t][:])
+        def quantize_w(h):
+            nc.vector.quantize_mx(out=w_codes[h][:].bitcast(E4M3X4), scales=w_scales[h][:], in_=w_bf[h][:])
 
-        def multiply(bank, t, first_col):
-            cols = slice(first_col, first_col + ITEMS)
+        def multiply(t):
+            cols = rows(t % 2)
             nc.tensor.matmul_mx(
-                out=bank[:],
-                lhsT=w_codes[t][:].bitcast(E4M3X4),
-                lhsT_scale=w_scales[t][:],
-                rhs=dz_codes[:, cols].bitcast(E5M2X4),
-                rhs_scale=dz_scales[:, cols],
+                out=de_psum[t][:],
+                lhsT=w_codes[t // 2][:, cols].bitcast(E4M3X4),
+                lhsT_scale=w_scales[t // 2][:, cols],
+                rhs=dz_codes[:].bitcast(E5M2X4),
+                rhs_scale=dz_scales[:],
                 start=True,
                 stop=True,
             )
 
-        def copy_de(target, t, first, last):
-            nc.scalar.copy(out=target[t][:, first:last], in_=de_psum[t][:, first:last])
+        def gather_v(got, tab, entries):
+            nc.vector.tensor_copy(got[:], tab[:].indirect(entries[:]))
 
-        def make_de(t):
-            quantize_w(t)
-            multiply(de_psum[t], t, HALF)
-            copy_de(de, t, 0, ITEMS)
+        def gather_s(got, tab, entries):
+            nc.scalar.activation(got[:], tab[:].indirect(entries[:]), COPY)
 
-        def gather_a(t):
-            nc.vector.tensor_copy(a_got[t][:], a_tab[t][:].indirect(a_list[:]))
+        def product(target, t, got):
+            nc.vector.tensor_tensor(target[:], de_psum[t][:], got[:], MULT)
 
-        def gather_b(t):
-            nc.vector.tensor_copy(b_got[t][:], b_tab[t][:].indirect(b_list[:]))
+        def put_v(out, window, entries, t, got):
+            nc.vector.tensor_tensor(window[:].indirect(entries[:]), de[t][:], got[:], MULT)
+            nc.sync.dma_start(out=out[rows(t), :], in_=window[:])
 
-        def scatter_0(t, first, last):
-            entries = a_list[:, first // LIST_STRIPE : last // LIST_STRIPE]
-            window = win_0[t % WINDOWS][:].indirect(entries)
-            nc.vector.tensor_tensor(window, de[t][:, first:last], b_got[t][:, first:last], MULT)
+        def put_s(out, window, entries, t, values):
+            for h in range(2):
+                part = entries[:, h * HALF // LIST_STRIPE : (h + 1) * HALF // LIST_STRIPE]
+                nc.scalar.activation(window[:].indirect(part), values[:, h * HALF : (h + 1) * HALF], COPY)
+            nc.sync.dma_start(out=out[rows(t), :], in_=window[:])
 
-        def put_0(t, first=0):
-            scatter_0(t, first, ITEMS)
-            nc.sync.dma_start(out=out_0[rows(t), :], in_=win_0[t % WINDOWS][:])
-
-        def put_1(t):
-            window = win_1[t % WINDOWS]
-            nc.vector.tensor_tensor(window[:].indirect(b_list[:]), de_late[t][:], a_got[t][:], MULT)
-            nc.sync.dma_start(out=out_1[rows(t), :], in_=window[:])
-
+        nc.sync.dma_start(b_list[:], joffs)
+        load_b(1)
+        load_b(0)
         load_w(0)
         load_dz(0)
-        nc.sync.dma_start(b_list[:], joffs)
-        load_b(0)
-        nc.sync.dma_start(a_list[:], offs)
-        load_b(1)
         load_dz(1)
-        load_b(2)
+        nc.sync.dma_start(a_list[:], offs)
         load_w(1)
         load_b(3)
-        load_w(2)
-        load_a(0)
+        load_b(2)
+        for t in (1, 0, 3, 2):
+            load_a(t)
 
-        nc.vector.memset(dz_codes[:, 0:HALF], 0)
-        nc.vector.memset(dz_scales[:, 0:HALF], 0)
-        for window in win_0 + win_1:
+        for window in win_0:
             nc.vector.memset(window[:].bitcast(I32), 0)
 
-        cast_w(0)
+        gather_s(b_got[1], b_tab[1], b_list)
+        gather_s(b_got[0], b_tab[0], b_list)
+        cast(nc.vector.tensor_copy, w_bf[0], w_raw[0], 0, PAIR)
+        cast(nc.vector.tensor_copy, dz_bf[0], dz_raw[0], 0, HALF)
         quantize_w(0)
-        interleave(nc.vector.tensor_copy, dz_bf[0][:, 0 : PACK * VECTOR_ITEMS], dz_raw[0][:, :, 0:VECTOR_ITEMS])
-        interleave(nc.scalar.copy, dz_bf[0][:, PACK * VECTOR_ITEMS :], dz_raw[0][:, :, VECTOR_ITEMS:])
         quantize_dz(0)
-        multiply(early_psum, 0, 0)
-        nc.scalar.copy(out=de[0][:, 0:HALF], in_=early_psum[:, HALF:ITEMS])
-        gather_b(0)
-        gather_b(1)
-        scatter_0(0, 0, HALF)
-
-        interleave(nc.scalar.copy, dz_bf[1][:], dz_raw[1][:])
-        cast_w(1)
+        cast(nc.vector.tensor_copy, dz_bf[1], dz_raw[1], 0, 160)
+        cast(nc.scalar.copy, dz_bf[1], dz_raw[1], 160, HALF)
         quantize_dz(1)
-        multiply(de_psum[0], 0, HALF)
-        copy_de(de, 0, HALF, ITEMS)
-        gather_b(2)
+        for window in win_1[0:2]:
+            nc.gpsimd.memset(window[:].bitcast(I32), 0)
+        multiply(1)
+        multiply(0)
+        product(da[1], 1, b_got[1])
+        nc.scalar.copy(out=de[0][:], in_=de_psum[0][:])
+        put_v(out_0, win_0[0], a_list, 0, b_got[0])
+        put_s(out_0, win_0[1], a_list, 1, da[1])
+
+        cast(nc.vector.tensor_copy, w_bf[1], w_raw[1], 0, PAIR)
         quantize_w(1)
-        multiply(de_psum[1], 1, HALF)
-        copy_de(de, 1, HELD, ITEMS)
-        gather_b(3)
-        put_0(0, first=HALF)
-        load_a(1)
-        load_w(3)
-        load_a(2)
+        for window in win_1[2:4]:
+            nc.gpsimd.memset(window[:].bitcast(I32), 0)
+        multiply(3)
+        multiply(2)
+        gather_s(b_got[3], b_tab[3], b_list)
+        gather_v(b_got[2], b_tab[2], b_list)
+        nc.scalar.copy(out=de[2][:], in_=de_psum[2][:])
+        product(da[3], 3, b_got[3])
+        gather_s(a_got[1], a_tab[1], a_list)
+        put_v(out_0, win_0[2], a_list, 2, b_got[2])
+        put_s(out_0, win_0[3], a_list, 3, da[3])
 
-        cast_w(2)
-        copy_de(de, 1, 0, HELD)
-        make_de(2)
-        put_0(1)
-        load_a(3)
-        copy_de(de_late, 0, 0, ITEMS - HELD)
-        copy_de(de_late, 1, HELD, ITEMS)
-        gather_a(0)
-        put_0(2)
-        gather_a(1)
+        product(db[1], 1, a_got[1])
+        gather_v(a_got[0], a_tab[0], a_list)
+        put_v(out_1, win_1[0], b_list, 0, a_got[0])
+        put_s(out_1, win_1[1], b_list, 1, db[1])
 
-        cast_w(3)
-        copy_de(de_late, 0, ITEMS - HELD, ITEMS)
-        copy_de(de_late, 1, 0, HELD)
-        make_de(3)
-        put_1(0)
-        put_1(1)
-        gather_a(2)
-        put_0(3)
-        gather_a(3)
-        put_1(2)
-        put_1(3)
+        gather_s(a_got[3], a_tab[3], a_list)
+        product(db[3], 3, a_got[3])
+        gather_v(a_got[2], a_tab[2], a_list)
+        put_v(out_1, win_1[2], b_list, 2, a_got[2])
+        put_s(out_1, win_1[3], b_list, 3, db[3])

@@ -41,55 +41,35 @@ def tile_attend_gqr_ab_kernel(tc, aT, bT, W, dz, offs, joffs, out_0, out_1):
 
         a_list = keep.tile([P, ITEMS // LIST_STRIPE], U16, name="a_list")
         b_list = keep.tile([P, ITEMS // LIST_STRIPE], U16, name="b_list")
-        dz_raw = [keep.tile([P, PACK, HALF], F32, name=f"dz_raw{h}") for h in range(2)]
-        w_raw = [keep.tile([P, PACK, PAIR], F32, name=f"w_raw{h}") for h in range(2)]
+        dz_raw = keep.tile([P, PACK, ITEMS], F32, name="dz_raw")
+        w_raw = keep.tile([P, PACK, D], F32, name="w_raw")
         a_tab = [keep.tile([P, A_COLS], F32, name=f"a_tab{t}") for t in range(D_TILES)]
         b_tab = [keep.tile([P, B_COLS], F32, name=f"b_tab{t}") for t in range(D_TILES)]
         win_0 = [keep.tile([P, A_COLS], F32, name=f"win_0_{t}") for t in range(D_TILES)]
-        win_1 = [shared.tile([P, B_COLS], F32, name=f"win_1_{t}", offset=4 * t * KIB) for t in range(D_TILES)]
-        dz_bf = [
-            keep.tile([P, HALF * PACK], BF16, name="dz_bf0", align_bytes=64),
-            shared.tile([P, HALF * PACK], BF16, name="dz_bf1", align_bytes=64, offset=3 * KIB),
-        ]
-        w_bf = [
-            keep.tile([P, PAIR * PACK], BF16, name="w_bf0", align_bytes=64),
-            shared.tile([P, PAIR * PACK], BF16, name="w_bf1", align_bytes=64, offset=11 * KIB),
-        ]
+        win_1 = [keep.tile([P, B_COLS], F32, name=f"win_1_{t}") for t in range(D_TILES)]
+        dz_bf = shared.tile([P, ITEMS * PACK], BF16, name="dz_bf", align_bytes=64, offset=0)
+        w_bf = [keep.tile([P, PAIR * PACK], BF16, name=f"w_bf{h}", align_bytes=64) for h in range(2)]
         dz_codes = keep.tile([P, ITEMS], U32, name="dz_codes", align_bytes=64)
         dz_scales = keep.tile([P, ITEMS], U8, name="dz_scales", align_bytes=64)
         w_codes = [keep.tile([P, PAIR], U32, name=f"w_codes{h}", align_bytes=64) for h in range(2)]
         w_scales = [keep.tile([P, PAIR], U8, name=f"w_scales{h}", align_bytes=64) for h in range(2)]
-        de = {t: keep.tile([P, ITEMS], F32, name=f"de{t}") for t in (0, 2)}
-        da = {t: keep.tile([P, ITEMS], F32, name=f"da{t}") for t in (1, 3)}
-        db = {t: keep.tile([P, ITEMS], F32, name=f"db{t}") for t in (1, 3)}
-        a_got = [keep.tile([P, ITEMS], F32, name=f"a_got{t}") for t in range(D_TILES)]
-        b_got = [keep.tile([P, ITEMS], F32, name=f"b_got{t}") for t in range(D_TILES)]
+        HELD = 16
+        got_s = keep.tile([P, ITEMS], F32, name="got_s")
+        held = keep.tile([P, 3 * ITEMS - 2 * HELD], F32, name="held")
+        de = {0: keep.tile([P, ITEMS], F32, name="de0")[:], 2: held[:, 2 * (ITEMS - HELD) :]}
+        da = {1: held[:, ITEMS - HELD : 2 * ITEMS - HELD], 3: keep.tile([P, ITEMS], F32, name="da3")[:]}
+        db = {t: keep.tile([P, ITEMS], F32, name=f"db{t}")[:] for t in (1, 2, 3)}
+        b_got = {0: shared.tile([P, ITEMS], F32, name="b_got0", offset=0)[:], 1: got_s[:], 3: got_s[:]}
+        b_got[2] = held[:, 0:ITEMS]
+        a_got = {t: keep.tile([P, ITEMS], F32, name=f"a_got{t}")[:] for t in (0, 2, 3)}
+        a_got[1] = held[:, 0:ITEMS]
         de_psum = [psum.tile([P, ITEMS], F32, name=f"de_psum{t}") for t in range(D_TILES)]
-
-        dz_rows = dz.rearrange("(p t) i -> p t i", t=PACK)
-        w_rows = W.rearrange("(p t) d -> p t d", t=PACK)
 
         def rows(t):
             return slice(t * P, (t + 1) * P)
 
-        def load_a(t):
-            nc.sync.dma_start(out=a_tab[t][:], in_=aT[rows(t), :])
-
-        def load_b(t):
-            nc.sync.dma_start(out=b_tab[t][:], in_=bT[rows(t), :])
-
-        def load_w(h):
-            nc.sync.dma_start(out=w_raw[h][:], in_=w_rows[:, :, h * PAIR : (h + 1) * PAIR])
-
-        def load_dz(h):
-            nc.sync.dma_start(out=dz_raw[h][:], in_=dz_rows[:, :, h * HALF : (h + 1) * HALF])
-
-        def cast(copy, grouped, raw, first, last):
-            interleave(copy, grouped[:, PACK * first : PACK * last], raw[:, :, first:last])
-
-        def quantize_dz(h):
-            cols = slice(h * HALF, (h + 1) * HALF)
-            nc.vector.quantize_mx(out=dz_codes[:, cols].bitcast(E5M2X4), scales=dz_scales[:, cols], in_=dz_bf[h][:])
+        def cast(copy, grouped, raw, first, last, at):
+            interleave(copy, grouped[:, PACK * at : PACK * (at + last - first)], raw[:, :, first:last])
 
         def quantize_w(h):
             nc.vector.quantize_mx(out=w_codes[h][:].bitcast(E4M3X4), scales=w_scales[h][:], in_=w_bf[h][:])
@@ -106,80 +86,80 @@ def tile_attend_gqr_ab_kernel(tc, aT, bT, W, dz, offs, joffs, out_0, out_1):
                 stop=True,
             )
 
+        def load_a(t):
+            nc.sync.dma_start(out=a_tab[t][:], in_=aT[rows(t), :])
+
+        def load_b(t):
+            nc.sync.dma_start(out=b_tab[t][:], in_=bT[rows(t), :])
+
         def gather_v(got, tab, entries):
-            nc.vector.tensor_copy(got[:], tab[:].indirect(entries[:]))
+            nc.vector.tensor_copy(got, tab[:].indirect(entries[:]))
 
         def gather_s(got, tab, entries):
-            nc.scalar.activation(got[:], tab[:].indirect(entries[:]), COPY)
+            nc.scalar.activation(got, tab[:].indirect(entries[:]), COPY)
 
         def product(target, t, got):
-            nc.vector.tensor_tensor(target[:], de_psum[t][:], got[:], MULT)
+            nc.vector.tensor_tensor(target, de_psum[t][:], got, MULT)
 
         def put_v(out, window, entries, t, got):
-            nc.vector.tensor_tensor(window[:].indirect(entries[:]), de[t][:], got[:], MULT)
+            nc.vector.tensor_tensor(window[:].indirect(entries[:]), de[t], got, MULT)
             nc.sync.dma_start(out=out[rows(t), :], in_=window[:])
 
-        def put_s(out, window, entries, t, values):
-            for h in range(2):
-                part = entries[:, h * HALF // LIST_STRIPE : (h + 1) * HALF // LIST_STRIPE]
-                nc.scalar.activation(window[:].indirect(part), values[:, h * HALF : (h + 1) * HALF], COPY)
+        def scatter_s(window, entries, values, h):
+            part = entries[:, h * HALF // LIST_STRIPE : (h + 1) * HALF // LIST_STRIPE]
+            nc.scalar.activation(window[:].indirect(part), values[:, h * HALF : (h + 1) * HALF], COPY)
+
+        def put_s(out, window, entries, t, values, first=0):
+            for h in range(first, 2):
+                scatter_s(window, entries, values, h)
             nc.sync.dma_start(out=out[rows(t), :], in_=window[:])
 
         nc.sync.dma_start(b_list[:], joffs)
         load_b(1)
-        load_b(0)
-        load_w(0)
-        load_dz(0)
-        load_dz(1)
+        nc.sync.dma_start(out=dz_raw[:], in_=dz.rearrange("(p t) i -> p t i", t=PACK))
+        nc.sync.dma_start(out=w_raw[:], in_=W.rearrange("(p t) d -> p t d", t=PACK))
         nc.sync.dma_start(a_list[:], offs)
-        load_w(1)
+        load_b(0)
         load_b(3)
+        load_a(1)
         load_b(2)
-        for t in (1, 0, 3, 2):
+        for t in (3, 2, 0):
             load_a(t)
 
-        for window in win_0:
+        for window in win_0 + win_1:
             nc.vector.memset(window[:].bitcast(I32), 0)
 
         gather_s(b_got[1], b_tab[1], b_list)
-        gather_s(b_got[0], b_tab[0], b_list)
-        cast(nc.vector.tensor_copy, w_bf[0], w_raw[0], 0, PAIR)
-        cast(nc.vector.tensor_copy, dz_bf[0], dz_raw[0], 0, HALF)
+        cast(nc.scalar.copy, dz_bf, dz_raw, 0, 384, 0)
+        cast(nc.vector.tensor_copy, dz_bf, dz_raw, 384, ITEMS, 384)
+        cast(nc.vector.tensor_copy, w_bf[0], w_raw, 0, P, 0)
+        cast(nc.scalar.copy, w_bf[0], w_raw, P, PAIR, P)
+        nc.vector.quantize_mx(out=dz_codes[:].bitcast(E5M2X4), scales=dz_scales[:], in_=dz_bf[:])
         quantize_w(0)
-        quantize_dz(0)
-        cast(nc.vector.tensor_copy, dz_bf[1], dz_raw[1], 0, 160)
-        cast(nc.scalar.copy, dz_bf[1], dz_raw[1], 160, HALF)
-        quantize_dz(1)
-        for window in win_1[0:2]:
-            nc.gpsimd.memset(window[:].bitcast(I32), 0)
         multiply(1)
         multiply(0)
-        product(da[1], 1, b_got[1])
-        nc.scalar.copy(out=de[0][:], in_=de_psum[0][:])
-        put_v(out_0, win_0[0], a_list, 0, b_got[0])
-        put_s(out_0, win_0[1], a_list, 1, da[1])
-
-        cast(nc.vector.tensor_copy, w_bf[1], w_raw[1], 0, PAIR)
+        cast(nc.scalar.copy, w_bf[1], w_raw, PAIR, D, 0)
+        gather_v(b_got[0], b_tab[0], b_list)
         quantize_w(1)
-        for window in win_1[2:4]:
-            nc.gpsimd.memset(window[:].bitcast(I32), 0)
         multiply(3)
         multiply(2)
+        product(da[1], 1, b_got[1])
+        nc.scalar.copy(out=de[0], in_=de_psum[0][:])
+        put_v(out_0, win_0[0], a_list, 0, b_got[0])
+        scatter_s(win_0[1], a_list, da[1], 0)
         gather_s(b_got[3], b_tab[3], b_list)
-        gather_v(b_got[2], b_tab[2], b_list)
-        nc.scalar.copy(out=de[2][:], in_=de_psum[2][:])
+        put_s(out_0, win_0[1], a_list, 1, da[1], first=1)
+        nc.scalar.copy(out=de[2], in_=de_psum[2][:])
+        gather_v(a_got[1], a_tab[1], a_list)
+        product(db[1], 1, a_got[1])
+        put_s(out_1, win_1[1], b_list, 1, db[1])
         product(da[3], 3, b_got[3])
-        gather_s(a_got[1], a_tab[1], a_list)
+        gather_v(b_got[2], b_tab[2], b_list)
         put_v(out_0, win_0[2], a_list, 2, b_got[2])
         put_s(out_0, win_0[3], a_list, 3, da[3])
-
-        product(db[1], 1, a_got[1])
+        for t in (3, 2):
+            gather_v(a_got[t], a_tab[t], a_list)
+            product(db[t], t, a_got[t])
+            put_s(out_1, win_1[t], b_list, t, db[t])
         gather_v(a_got[0], a_tab[0], a_list)
         put_v(out_1, win_1[0], b_list, 0, a_got[0])
-        put_s(out_1, win_1[1], b_list, 1, db[1])
-
-        gather_s(a_got[3], a_tab[3], a_list)
-        product(db[3], 3, a_got[3])
-        gather_v(a_got[2], a_tab[2], a_list)
-        put_v(out_1, win_1[2], b_list, 2, a_got[2])
-        put_s(out_1, win_1[3], b_list, 3, db[3])

@@ -41,47 +41,60 @@ def tile_attend_gqr_ab_kernel(tc, aT, bT, W, dz, offs, joffs, out_0, out_1):
 
         a_list = keep.tile([P, ITEMS // LIST_STRIPE], U16, name="a_list")
         b_list = keep.tile([P, ITEMS // LIST_STRIPE], U16, name="b_list")
-        dz_raw = keep.tile([P, PACK, ITEMS], F32, name="dz_raw")
-        w_raw = keep.tile([P, PACK, D], F32, name="w_raw")
+        def on(name, shape, dtype, kib):
+            return shared.tile(shape, dtype, name=name, align_bytes=64, offset=kib * KIB)
+
+        dz_raw = [keep.tile([P, PACK, HALF], F32, name=f"dz_raw{h}") for h in range(2)]
+        w_raw = [keep.tile([P, PACK, PAIR], F32, name="w_raw0"), on("w_raw1", [P, PACK, PAIR], F32, 34)]
         a_tab = [keep.tile([P, A_COLS], F32, name=f"a_tab{t}") for t in range(D_TILES)]
         b_tab = [keep.tile([P, B_COLS], F32, name=f"b_tab{t}") for t in range(D_TILES)]
-        win_0 = [keep.tile([P, A_COLS], F32, name=f"win_0_{t}") for t in range(D_TILES)]
-        win_1 = [keep.tile([P, B_COLS], F32, name=f"win_1_{t}") for t in range(D_TILES)]
-        dz_bf = shared.tile([P, ITEMS * PACK], BF16, name="dz_bf", align_bytes=64, offset=0)
-        w_bf = [keep.tile([P, PAIR * PACK], BF16, name=f"w_bf{h}", align_bytes=64) for h in range(2)]
+        win_0 = [keep.tile([P, A_COLS], F32, name=f"win_0_{t}") for t in range(2)]
+        win_0 = win_0 + [on("win_0_2", [P, A_COLS], F32, 0), on("win_0_3", [P, A_COLS], F32, 14)]
+        win_1 = [on(f"win_1_{t}", [P, B_COLS], F32, at) for t, at in enumerate((10, 22, 26, 30))]
+        dz_bf = [keep.tile([P, HALF * PACK], BF16, name="dz_bf0", align_bytes=64), on("dz_bf1", [P, HALF * PACK], BF16, 7)]
+        w_bf = [on("w_bf0", [P, PAIR * PACK], BF16, 7), on("w_bf1", [P, PAIR * PACK], BF16, 13)]
         dz_codes = keep.tile([P, ITEMS], U32, name="dz_codes", align_bytes=64)
         dz_scales = keep.tile([P, ITEMS], U8, name="dz_scales", align_bytes=64)
         w_codes = [keep.tile([P, PAIR], U32, name=f"w_codes{h}", align_bytes=64) for h in range(2)]
         w_scales = [keep.tile([P, PAIR], U8, name=f"w_scales{h}", align_bytes=64) for h in range(2)]
-        HELD = 16
-        got_s = keep.tile([P, ITEMS], F32, name="got_s")
-        held = keep.tile([P, 3 * ITEMS - 2 * HELD], F32, name="held")
-        de = {0: keep.tile([P, ITEMS], F32, name="de0")[:], 2: held[:, 2 * (ITEMS - HELD) :]}
-        da = {1: held[:, ITEMS - HELD : 2 * ITEMS - HELD], 3: keep.tile([P, ITEMS], F32, name="da3")[:]}
-        db = {t: keep.tile([P, ITEMS], F32, name=f"db{t}")[:] for t in (1, 2, 3)}
-        b_got = {0: shared.tile([P, ITEMS], F32, name="b_got0", offset=0)[:], 1: got_s[:], 3: got_s[:]}
-        b_got[2] = held[:, 0:ITEMS]
-        a_got = {t: keep.tile([P, ITEMS], F32, name=f"a_got{t}")[:] for t in (0, 2, 3)}
-        a_got[1] = held[:, 0:ITEMS]
+        de_3 = keep.tile([P, ITEMS], F32, name="de_3")
+        da = [keep.tile([P, ITEMS], F32, name="da0"), on("da1", [P, ITEMS], F32, 25), on("da2", [P, ITEMS], F32, 30)]
+        db = [keep.tile([P, ITEMS], F32, name=f"db{t}") for t in range(3)]
+        got_x = on("got_x", [P, ITEMS], F32, 34)
+        got_y = keep.tile([P, ITEMS], F32, name="got_y")
+        b_got = [on("b_got0", [P, ITEMS], F32, 13), on("b_got1", [P, ITEMS], F32, 8), got_x, got_y]
+        a_got = [got_y, got_x, got_x, got_y]
         de_psum = [psum.tile([P, ITEMS], F32, name=f"de_psum{t}") for t in range(D_TILES)]
 
         def rows(t):
             return slice(t * P, (t + 1) * P)
 
-        def cast(copy, grouped, raw, first, last, at):
-            interleave(copy, grouped[:, PACK * at : PACK * (at + last - first)], raw[:, :, first:last])
+        def half(h):
+            return slice(h * HALF, (h + 1) * HALF)
+
+        def cast(copy, grouped, raw, first, last):
+            interleave(copy, grouped[:, PACK * first : PACK * last], raw[:, :, first:last])
+
+        def cast_shared(grouped, raw):
+            cast(nc.vector.tensor_copy, grouped, raw, 0, 160)
+            cast(nc.scalar.copy, grouped, raw, 160, HALF)
+
+        def quantize_dz(h):
+            nc.vector.quantize_mx(
+                out=dz_codes[:, half(h)].bitcast(E5M2X4), scales=dz_scales[:, half(h)], in_=dz_bf[h][:]
+            )
 
         def quantize_w(h):
             nc.vector.quantize_mx(out=w_codes[h][:].bitcast(E4M3X4), scales=w_scales[h][:], in_=w_bf[h][:])
 
-        def multiply(t):
+        def multiply(t, items):
             cols = rows(t % 2)
             nc.tensor.matmul_mx(
-                out=de_psum[t][:],
+                out=de_psum[t][:, items],
                 lhsT=w_codes[t // 2][:, cols].bitcast(E4M3X4),
                 lhsT_scale=w_scales[t // 2][:, cols],
-                rhs=dz_codes[:].bitcast(E5M2X4),
-                rhs_scale=dz_scales[:],
+                rhs=dz_codes[:, items].bitcast(E5M2X4),
+                rhs_scale=dz_scales[:, items],
                 start=True,
                 stop=True,
             )
@@ -92,74 +105,98 @@ def tile_attend_gqr_ab_kernel(tc, aT, bT, W, dz, offs, joffs, out_0, out_1):
         def load_b(t):
             nc.sync.dma_start(out=b_tab[t][:], in_=bT[rows(t), :])
 
-        def gather_v(got, tab, entries):
-            nc.vector.tensor_copy(got, tab[:].indirect(entries[:]))
+        def load_w(h):
+            nc.sync.dma_start(out=w_raw[h][:], in_=W.rearrange("(p t) d -> p t d", t=PACK)[:, :, half(h)])
 
-        def gather_s(got, tab, entries):
-            nc.scalar.activation(got, tab[:].indirect(entries[:]), COPY)
+        def load_dz(h):
+            nc.sync.dma_start(out=dz_raw[h][:], in_=dz.rearrange("(p t) i -> p t i", t=PACK)[:, :, half(h)])
 
-        def product(target, t, got):
-            nc.vector.tensor_tensor(target, de_psum[t][:], got, MULT)
+        def part_of(entries, h):
+            return entries[:, h * HALF // LIST_STRIPE : (h + 1) * HALF // LIST_STRIPE]
 
-        def put_v(out, window, entries, t, got):
-            nc.vector.tensor_tensor(window[:].indirect(entries[:]), de[t], got, MULT)
-            nc.sync.dma_start(out=out[rows(t), :], in_=window[:])
+        def gather(got, tab, entries):
+            nc.vector.tensor_copy(got[:], tab[:].indirect(entries[:]))
+
+        def product(target, t, got, items):
+            nc.vector.tensor_tensor(target[:, items], de_psum[t][:, items], got[:, items], MULT)
+
+        def put_v(out, window, entries, got):
+            nc.vector.tensor_tensor(window[:].indirect(entries[:]), de_3[:], got[:], MULT)
+            nc.sync.dma_start(out=out[rows(3), :], in_=window[:])
 
         def scatter_s(window, entries, values, h):
             part = entries[:, h * HALF // LIST_STRIPE : (h + 1) * HALF // LIST_STRIPE]
-            nc.scalar.activation(window[:].indirect(part), values[:, h * HALF : (h + 1) * HALF], COPY)
+            nc.scalar.activation(window[:].indirect(part), values[:, half(h)], COPY)
 
         def put_s(out, window, entries, t, values, first=0):
             for h in range(first, 2):
                 scatter_s(window, entries, values, h)
             nc.sync.dma_start(out=out[rows(t), :], in_=window[:])
 
-        nc.sync.dma_start(b_list[:], joffs)
-        load_b(1)
-        nc.sync.dma_start(out=dz_raw[:], in_=dz.rearrange("(p t) i -> p t i", t=PACK))
-        nc.sync.dma_start(out=w_raw[:], in_=W.rearrange("(p t) d -> p t d", t=PACK))
-        nc.sync.dma_start(a_list[:], offs)
-        load_b(0)
-        load_b(3)
-        load_a(1)
-        load_b(2)
-        for t in (3, 2, 0):
-            load_a(t)
+        def clear(window):
+            nc.gpsimd.memset(window[:].bitcast(I32), 0)
 
-        for window in win_0 + win_1:
+        every = slice(0, ITEMS)
+
+        load_dz(0)
+        nc.sync.dma_start(b_list[:], joffs)
+        load_b(0)
+        load_w(0)
+        nc.sync.dma_start(a_list[:], offs)
+        load_dz(1)
+        load_b(1)
+        load_w(1)
+        load_b(2)
+        load_a(0)
+        load_a(1)
+        load_b(3)
+        load_a(2)
+        load_a(3)
+
+        for window in win_0[0:2]:
             nc.vector.memset(window[:].bitcast(I32), 0)
 
-        gather_s(b_got[1], b_tab[1], b_list)
-        cast(nc.scalar.copy, dz_bf, dz_raw, 0, 384, 0)
-        cast(nc.vector.tensor_copy, dz_bf, dz_raw, 384, ITEMS, 384)
-        cast(nc.vector.tensor_copy, w_bf[0], w_raw, 0, P, 0)
-        cast(nc.scalar.copy, w_bf[0], w_raw, P, PAIR, P)
-        nc.vector.quantize_mx(out=dz_codes[:].bitcast(E5M2X4), scales=dz_scales[:], in_=dz_bf[:])
+        cast(nc.scalar.copy, dz_bf[0], dz_raw[0], 0, HALF)
+        nc.scalar.activation(b_got[0][:], b_tab[0][:].indirect(b_list[:]), COPY)
+        quantize_dz(0)
+        cast(nc.vector.tensor_copy, w_bf[0], w_raw[0], 0, 192)
+        cast(nc.scalar.copy, w_bf[0], w_raw[0], 192, PAIR)
         quantize_w(0)
-        multiply(1)
-        multiply(0)
-        cast(nc.scalar.copy, w_bf[1], w_raw, PAIR, D, 0)
-        gather_v(b_got[0], b_tab[0], b_list)
+        multiply(0, half(0))
+        cast_shared(dz_bf[1], dz_raw[1])
+        product(da[0], 0, b_got[0], half(0))
+        scatter_s(win_0[0], a_list, da[0], 0)
+        quantize_dz(1)
+        clear(win_0[2])
+        multiply(0, half(1))
+        multiply(1, every)
+        nc.vector.tensor_copy(b_got[1][:, half(0)], b_tab[1][:].indirect(part_of(b_list, 0)))
+        product(da[0], 0, b_got[0], half(1))
+        nc.vector.tensor_copy(b_got[1][:, half(1)], b_tab[1][:].indirect(part_of(b_list, 1)))
+        put_s(out_0, win_0[0], a_list, 0, da[0], first=1)
+        product(da[1], 1, b_got[1], every)
+        put_s(out_0, win_0[1], a_list, 1, da[1])
+        cast(nc.vector.tensor_copy, w_bf[1], w_raw[1], 0, PAIR)
         quantize_w(1)
-        multiply(3)
-        multiply(2)
-        product(da[1], 1, b_got[1])
-        nc.scalar.copy(out=de[0], in_=de_psum[0][:])
-        put_v(out_0, win_0[0], a_list, 0, b_got[0])
-        scatter_s(win_0[1], a_list, da[1], 0)
-        gather_s(b_got[3], b_tab[3], b_list)
-        put_s(out_0, win_0[1], a_list, 1, da[1], first=1)
-        nc.scalar.copy(out=de[2], in_=de_psum[2][:])
-        gather_v(a_got[1], a_tab[1], a_list)
-        product(db[1], 1, a_got[1])
-        put_s(out_1, win_1[1], b_list, 1, db[1])
-        product(da[3], 3, b_got[3])
-        gather_v(b_got[2], b_tab[2], b_list)
-        put_v(out_0, win_0[2], a_list, 2, b_got[2])
-        put_s(out_0, win_0[3], a_list, 3, da[3])
-        for t in (3, 2):
-            gather_v(a_got[t], a_tab[t], a_list)
-            product(db[t], t, a_got[t])
+        clear(win_1[0])
+        clear(win_0[3])
+        multiply(2, every)
+        multiply(3, every)
+        nc.scalar.copy(out=de_3[:], in_=de_psum[3][:])
+        gather(b_got[2], b_tab[2], b_list)
+        product(da[2], 2, b_got[2], every)
+        clear(win_1[1])
+        clear(win_1[2])
+        put_s(out_0, win_0[2], a_list, 2, da[2])
+        clear(win_1[3])
+        for t in range(2):
+            gather(a_got[t], a_tab[t], a_list)
+            product(db[t], t, a_got[t], every)
             put_s(out_1, win_1[t], b_list, t, db[t])
-        gather_v(a_got[0], a_tab[0], a_list)
-        put_v(out_1, win_1[0], b_list, 0, a_got[0])
+        gather(b_got[3], b_tab[3], b_list)
+        put_v(out_0, win_0[3], a_list, b_got[3])
+        gather(a_got[2], a_tab[2], a_list)
+        product(db[2], 2, a_got[2], every)
+        put_s(out_1, win_1[2], b_list, 2, db[2])
+        gather(a_got[3], a_tab[3], a_list)
+        put_v(out_1, win_1[3], b_list, a_got[3])

@@ -39,32 +39,33 @@ def tile_attend_gqr_ab_kernel(tc, aT, bT, W, dz, offs, joffs, out_0, out_1):
         shared = ctx.enter_context(tc.tile_pool(name="shared", bufs=1))
         psum = ctx.enter_context(tc.psum_pool(name="psum", bufs=1))
 
-        a_list = keep.tile([P, ITEMS // LIST_STRIPE], U16, name="a_list")
-        b_list = keep.tile([P, ITEMS // LIST_STRIPE], U16, name="b_list")
         def on(name, shape, dtype, kib):
             return shared.tile(shape, dtype, name=name, align_bytes=64, offset=kib * KIB)
 
+        a_list = keep.tile([P, ITEMS // LIST_STRIPE], U16, name="a_list")
+        b_list = keep.tile([P, ITEMS // LIST_STRIPE], U16, name="b_list")
         dz_raw = [keep.tile([P, PACK, HALF], F32, name=f"dz_raw{h}") for h in range(2)]
-        w_raw = [keep.tile([P, PACK, PAIR], F32, name="w_raw0"), on("w_raw1", [P, PACK, PAIR], F32, 34)]
-        a_tab = [keep.tile([P, A_COLS], F32, name=f"a_tab{t}") for t in range(D_TILES)]
+        w_raw = [keep.tile([P, PACK, PAIR], F32, name=f"w_raw{h}") for h in range(2)]
+        a_tab = [keep.tile([P, A_COLS], F32, name=f"a_tab{t}") for t in range(2)]
+        a_tab = a_tab + [on("a_tab2", [P, A_COLS], F32, 24), keep.tile([P, A_COLS], F32, name="a_tab3")]
         b_tab = [keep.tile([P, B_COLS], F32, name=f"b_tab{t}") for t in range(D_TILES)]
-        win_0 = [keep.tile([P, A_COLS], F32, name=f"win_0_{t}") for t in range(2)]
-        win_0 = win_0 + [on("win_0_2", [P, A_COLS], F32, 0), on("win_0_3", [P, A_COLS], F32, 14)]
-        win_1 = [on(f"win_1_{t}", [P, B_COLS], F32, at) for t, at in enumerate((10, 22, 26, 30))]
-        dz_bf = [keep.tile([P, HALF * PACK], BF16, name="dz_bf0", align_bytes=64), on("dz_bf1", [P, HALF * PACK], BF16, 7)]
-        w_bf = [on("w_bf0", [P, PAIR * PACK], BF16, 7), on("w_bf1", [P, PAIR * PACK], BF16, 13)]
+        win_0 = [keep.tile([P, A_COLS], F32, name=f"win_0_{t}") for t in range(3)]
+        win_0 = win_0 + [on("win_0_3", [P, A_COLS], F32, 4)]
+        win_1 = [on(f"win_1_{t}", [P, B_COLS], F32, at) for t, at in enumerate((0, 12, 16, 20))]
+        dz_bf = [keep.tile([P, HALF * PACK], BF16, name=f"dz_bf{h}", align_bytes=64) for h in range(2)]
+        w_bf = [keep.tile([P, PAIR * PACK], BF16, name="w_bf0", align_bytes=64), on("w_bf1", [P, PAIR * PACK], BF16, 3)]
         dz_codes = keep.tile([P, ITEMS], U32, name="dz_codes", align_bytes=64)
         dz_scales = keep.tile([P, ITEMS], U8, name="dz_scales", align_bytes=64)
         w_codes = [keep.tile([P, PAIR], U32, name=f"w_codes{h}", align_bytes=64) for h in range(2)]
         w_scales = [keep.tile([P, PAIR], U8, name=f"w_scales{h}", align_bytes=64) for h in range(2)]
         de_3 = keep.tile([P, ITEMS], F32, name="de_3")
-        da = [keep.tile([P, ITEMS], F32, name="da0"), on("da1", [P, ITEMS], F32, 25), on("da2", [P, ITEMS], F32, 30)]
-        db = [keep.tile([P, ITEMS], F32, name=f"db{t}") for t in range(3)]
-        got_x = on("got_x", [P, ITEMS], F32, 34)
-        got_y = keep.tile([P, ITEMS], F32, name="got_y")
-        b_got = [on("b_got0", [P, ITEMS], F32, 13), on("b_got1", [P, ITEMS], F32, 8), got_x, got_y]
-        a_got = [got_y, got_x, got_x, got_y]
-        de_psum = [psum.tile([P, ITEMS], F32, name=f"de_psum{t}") for t in range(D_TILES)]
+        UNITS = 6
+        got = keep.tile([P, UNITS * ITEMS], F32, name="got")
+        got_3 = [on("got_3_0", [P, ITEMS], F32, 24), keep.tile([P, ITEMS], F32, name="got_3_1")]
+        values = [keep.tile([P, ITEMS], F32, name=f"values{k}") for k in range(2)]
+        values = values + [on("values2", [P, ITEMS], F32, 15), on("values3", [P, ITEMS], F32, 20)]
+        values = values + [keep.tile([P, ITEMS], F32, name=f"values{k}") for k in range(4, UNITS + 1)]
+        banks = [psum.tile([P, ITEMS], F32, name=f"bank{t}") for t in range(D_TILES)]
 
         def rows(t):
             return slice(t * P, (t + 1) * P)
@@ -72,12 +73,11 @@ def tile_attend_gqr_ab_kernel(tc, aT, bT, W, dz, offs, joffs, out_0, out_1):
         def half(h):
             return slice(h * HALF, (h + 1) * HALF)
 
+        def part_of(entries, h):
+            return entries[:, h * HALF // LIST_STRIPE : (h + 1) * HALF // LIST_STRIPE]
+
         def cast(copy, grouped, raw, first, last):
             interleave(copy, grouped[:, PACK * first : PACK * last], raw[:, :, first:last])
-
-        def cast_shared(grouped, raw):
-            cast(nc.vector.tensor_copy, grouped, raw, 0, 160)
-            cast(nc.scalar.copy, grouped, raw, 160, HALF)
 
         def quantize_dz(h):
             nc.vector.quantize_mx(
@@ -87,10 +87,10 @@ def tile_attend_gqr_ab_kernel(tc, aT, bT, W, dz, offs, joffs, out_0, out_1):
         def quantize_w(h):
             nc.vector.quantize_mx(out=w_codes[h][:].bitcast(E4M3X4), scales=w_scales[h][:], in_=w_bf[h][:])
 
-        def multiply(t, items):
+        def multiply(out, t, items):
             cols = rows(t % 2)
             nc.tensor.matmul_mx(
-                out=de_psum[t][:, items],
+                out=out,
                 lhsT=w_codes[t // 2][:, cols].bitcast(E4M3X4),
                 lhsT_scale=w_scales[t // 2][:, cols],
                 rhs=dz_codes[:, items].bitcast(E5M2X4),
@@ -98,6 +98,9 @@ def tile_attend_gqr_ab_kernel(tc, aT, bT, W, dz, offs, joffs, out_0, out_1):
                 start=True,
                 stop=True,
             )
+
+        def multiply_half(t, h):
+            multiply(banks[(t + h - 1) % 3][:, half(1 - h)], t, half(h))
 
         def load_a(t):
             nc.sync.dma_start(out=a_tab[t][:], in_=aT[rows(t), :])
@@ -111,32 +114,47 @@ def tile_attend_gqr_ab_kernel(tc, aT, bT, W, dz, offs, joffs, out_0, out_1):
         def load_dz(h):
             nc.sync.dma_start(out=dz_raw[h][:], in_=dz.rearrange("(p t) i -> p t i", t=PACK)[:, :, half(h)])
 
-        def part_of(entries, h):
-            return entries[:, h * HALF // LIST_STRIPE : (h + 1) * HALF // LIST_STRIPE]
+        tabs = b_tab[0:3] + a_tab[0:3]
+        gather_lists = [b_list] * 3 + [a_list] * 3
+        scatter_lists = [a_list] * 3 + [b_list] * 3
+        wins = win_0[0:3] + win_1[0:3]
+        outs = [out_0] * 3 + [out_1] * 3
 
-        def gather(got, tab, entries):
-            nc.vector.tensor_copy(got[:], tab[:].indirect(entries[:]))
+        def gather(k):
+            nc.vector.tensor_copy(got[:, k * ITEMS : (k + 1) * ITEMS], tabs[k][:].indirect(gather_lists[k][:]))
 
-        def product(target, t, got, items):
-            nc.vector.tensor_tensor(target[:, items], de_psum[t][:, items], got[:, items], MULT)
+        def gather_half(k, h):
+            at = k * ITEMS + h * HALF
+            nc.vector.tensor_copy(got[:, at : at + HALF], tabs[k][:].indirect(part_of(gather_lists[k], h)))
 
-        def put_v(out, window, entries, got):
-            nc.vector.tensor_tensor(window[:].indirect(entries[:]), de_3[:], got[:], MULT)
+        def product(k):
+            first = HALF if k == 0 else 0
+            last = HALF if k == UNITS else ITEMS
+            at = k * ITEMS - HALF
+            nc.vector.tensor_tensor(
+                values[k][:, first:last], banks[(k - 1) % 3][:, first:last], got[:, at + first : at + last], MULT
+            )
+
+        def scatter(k, h):
+            nc.scalar.activation(
+                wins[k][:].indirect(part_of(scatter_lists[k], h)), values[k + h][:, half(1 - h)], COPY
+            )
+
+        def step(k, made=False):
+            if not made:
+                product(k)
+            if k < UNITS:
+                scatter(k, 0)
+            if k > 0:
+                scatter(k - 1, 1)
+                nc.sync.dma_start(out=outs[k - 1][rows((k - 1) % 3), :], in_=wins[k - 1][:])
+
+        def put_v(out, window, entries, gathered):
+            nc.vector.tensor_tensor(window[:].indirect(entries[:]), de_3[:], gathered[:], MULT)
             nc.sync.dma_start(out=out[rows(3), :], in_=window[:])
-
-        def scatter_s(window, entries, values, h):
-            part = entries[:, h * HALF // LIST_STRIPE : (h + 1) * HALF // LIST_STRIPE]
-            nc.scalar.activation(window[:].indirect(part), values[:, half(h)], COPY)
-
-        def put_s(out, window, entries, t, values, first=0):
-            for h in range(first, 2):
-                scatter_s(window, entries, values, h)
-            nc.sync.dma_start(out=out[rows(t), :], in_=window[:])
 
         def clear(window):
             nc.gpsimd.memset(window[:].bitcast(I32), 0)
-
-        every = slice(0, ITEMS)
 
         load_dz(0)
         nc.sync.dma_start(b_list[:], joffs)
@@ -153,50 +171,48 @@ def tile_attend_gqr_ab_kernel(tc, aT, bT, W, dz, offs, joffs, out_0, out_1):
         load_a(2)
         load_a(3)
 
-        for window in win_0[0:2]:
+        for window in win_0[0:3]:
             nc.vector.memset(window[:].bitcast(I32), 0)
 
         cast(nc.scalar.copy, dz_bf[0], dz_raw[0], 0, HALF)
-        nc.scalar.activation(b_got[0][:], b_tab[0][:].indirect(b_list[:]), COPY)
+        nc.scalar.activation(got[:, 0:ITEMS], b_tab[0][:].indirect(b_list[:]), COPY)
         quantize_dz(0)
         cast(nc.vector.tensor_copy, w_bf[0], w_raw[0], 0, 192)
         cast(nc.scalar.copy, w_bf[0], w_raw[0], 192, PAIR)
         quantize_w(0)
-        multiply(0, half(0))
-        cast_shared(dz_bf[1], dz_raw[1])
-        product(da[0], 0, b_got[0], half(0))
-        scatter_s(win_0[0], a_list, da[0], 0)
+        multiply_half(0, 0)
+        multiply_half(1, 0)
+        cast(nc.vector.tensor_copy, dz_bf[1], dz_raw[1], 0, 160)
+        cast(nc.scalar.copy, dz_bf[1], dz_raw[1], 160, HALF)
+        step(0)
         quantize_dz(1)
-        clear(win_0[2])
-        multiply(0, half(1))
-        multiply(1, every)
-        nc.vector.tensor_copy(b_got[1][:, half(0)], b_tab[1][:].indirect(part_of(b_list, 0)))
-        product(da[0], 0, b_got[0], half(1))
-        nc.vector.tensor_copy(b_got[1][:, half(1)], b_tab[1][:].indirect(part_of(b_list, 1)))
-        put_s(out_0, win_0[0], a_list, 0, da[0], first=1)
-        product(da[1], 1, b_got[1], every)
-        put_s(out_0, win_0[1], a_list, 1, da[1])
+        multiply_half(0, 1)
+        multiply_half(1, 1)
+        gather_half(1, 0)
+        step(1)
         cast(nc.vector.tensor_copy, w_bf[1], w_raw[1], 0, PAIR)
+        gather_half(1, 1)
         quantize_w(1)
         clear(win_1[0])
         clear(win_0[3])
-        multiply(2, every)
-        multiply(3, every)
-        nc.scalar.copy(out=de_3[:], in_=de_psum[3][:])
-        gather(b_got[2], b_tab[2], b_list)
-        product(da[2], 2, b_got[2], every)
+        multiply_half(2, 0)
+        multiply_half(2, 1)
+        multiply(banks[3][:], 3, slice(0, ITEMS))
+        gather(2)
+        step(2)
+        nc.scalar.copy(out=de_3[:], in_=banks[3][:])
         clear(win_1[1])
         clear(win_1[2])
-        put_s(out_0, win_0[2], a_list, 2, da[2])
+        gather(3)
+        step(3)
         clear(win_1[3])
-        for t in range(2):
-            gather(a_got[t], a_tab[t], a_list)
-            product(db[t], t, a_got[t], every)
-            put_s(out_1, win_1[t], b_list, t, db[t])
-        gather(b_got[3], b_tab[3], b_list)
-        put_v(out_0, win_0[3], a_list, b_got[3])
-        gather(a_got[2], a_tab[2], a_list)
-        product(db[2], 2, a_got[2], every)
-        put_s(out_1, win_1[2], b_list, 2, db[2])
-        gather(a_got[3], a_tab[3], a_list)
-        put_v(out_1, win_1[3], b_list, a_got[3])
+        gather(4)
+        step(4)
+        gather(5)
+        nc.vector.tensor_copy(got_3[0][:], b_tab[3][:].indirect(b_list[:]))
+        product(5)
+        put_v(out_0, win_0[3], a_list, got_3[0])
+        step(5, made=True)
+        step(6)
+        nc.vector.tensor_copy(got_3[1][:], a_tab[3][:].indirect(a_list[:]))
+        put_v(out_1, win_1[3], b_list, got_3[1])

@@ -42,29 +42,33 @@ def tile_attend_gqr_ab_kernel(tc, aT, bT, W, dz, offs, joffs, out_0, out_1):
         def on(name, shape, dtype, kib):
             return shared.tile(shape, dtype, name=name, align_bytes=64, offset=kib * KIB)
 
+        UNITS = 6
         a_list = keep.tile([P, ITEMS // LIST_STRIPE], U16, name="a_list")
         b_list = keep.tile([P, ITEMS // LIST_STRIPE], U16, name="b_list")
-        dz_raw = [keep.tile([P, PACK, HALF], F32, name=f"dz_raw{h}") for h in range(2)]
-        w_raw = [keep.tile([P, PACK, PAIR], F32, name=f"w_raw{h}") for h in range(2)]
-        a_tab = [keep.tile([P, A_COLS], F32, name=f"a_tab{t}") for t in range(2)]
-        a_tab = a_tab + [on("a_tab2", [P, A_COLS], F32, 24), keep.tile([P, A_COLS], F32, name="a_tab3")]
-        b_tab = [keep.tile([P, B_COLS], F32, name=f"b_tab{t}") for t in range(D_TILES)]
-        win_0 = [keep.tile([P, A_COLS], F32, name=f"win_0_{t}") for t in range(3)]
-        win_0 = win_0 + [on("win_0_3", [P, A_COLS], F32, 4)]
-        win_1 = [on(f"win_1_{t}", [P, B_COLS], F32, at) for t, at in enumerate((0, 12, 16, 20))]
-        dz_bf = [keep.tile([P, HALF * PACK], BF16, name=f"dz_bf{h}", align_bytes=64) for h in range(2)]
-        w_bf = [keep.tile([P, PAIR * PACK], BF16, name="w_bf0", align_bytes=64), on("w_bf1", [P, PAIR * PACK], BF16, 3)]
+        dz_raw = keep.tile([P, PACK, ITEMS], F32, name="dz_raw")
+        w_raw = keep.tile([P, PACK, D], F32, name="w_raw")
+        a_pair = keep.tile([P, 2 * A_COLS], F32, name="a_pair")
+        a_tab = [a_pair[:, 0:A_COLS], a_pair[:, A_COLS:]]
+        a_tab = a_tab + [on(f"a_tab{t}", [P, A_COLS], F32, 16 + 8 * t)[:] for t in (2, 3)]
+        b_pair = on("b_pair", [P, 2 * B_COLS], F32, 24)
+        b_tab = [keep.tile([P, B_COLS], F32, name=f"b_tab{t}")[:] for t in range(2)]
+        b_tab = b_tab + [b_pair[:, 0:B_COLS], b_pair[:, B_COLS:]]
+        win_0 = [keep.tile([P, A_COLS], F32, name=f"win_0_{t}") for t in range(2)]
+        win_0 = win_0 + [on("win_0_2", [P, A_COLS], F32, 48), on("win_0_3", [P, A_COLS], F32, 56)]
+        win_1 = [on(f"win_1_{t}", [P, B_COLS], F32, 8 + 4 * t) for t in range(D_TILES)]
+        dz_bf = keep.tile([P, ITEMS * PACK], BF16, name="dz_bf", align_bytes=64)
+        w_bf = [keep.tile([P, PAIR * PACK], BF16, name="w_bf0", align_bytes=64), on("w_bf1", [P, PAIR * PACK], BF16, 55)]
         dz_codes = keep.tile([P, ITEMS], U32, name="dz_codes", align_bytes=64)
         dz_scales = keep.tile([P, ITEMS], U8, name="dz_scales", align_bytes=64)
-        w_codes = [keep.tile([P, PAIR], U32, name=f"w_codes{h}", align_bytes=64) for h in range(2)]
-        w_scales = [keep.tile([P, PAIR], U8, name=f"w_scales{h}", align_bytes=64) for h in range(2)]
-        de_3 = keep.tile([P, ITEMS], F32, name="de_3")
-        UNITS = 6
+        w_codes = keep.tile([P, D], U32, name="w_codes", align_bytes=64)
+        w_scales = keep.tile([P, D], U8, name="w_scales", align_bytes=64)
+        de = {2: on("de2", [P, ITEMS], F32, 24), 3: on("de3", [P, ITEMS], F32, 26)}
         got = keep.tile([P, UNITS * ITEMS], F32, name="got")
-        got_3 = [on("got_3_0", [P, ITEMS], F32, 24), keep.tile([P, ITEMS], F32, name="got_3_1")]
-        values = [keep.tile([P, ITEMS], F32, name=f"values{k}") for k in range(2)]
-        values = values + [on("values2", [P, ITEMS], F32, 15), on("values3", [P, ITEMS], F32, 20)]
-        values = values + [keep.tile([P, ITEMS], F32, name=f"values{k}") for k in range(4, UNITS + 1)]
+        got_v = {t: keep.tile([P, ITEMS], F32, name=f"got_v{t}") for t in (2, 3)}
+        values = [keep.tile([P, ITEMS], F32, name="values0")]
+        values = values + [on("values1", [P, ITEMS], F32, 11), on("values2", [P, ITEMS], F32, 19)]
+        values = values + [keep.tile([P, ITEMS], F32, name=f"values{k}") for k in (3, 4)]
+        values = values + [on("values5", [P, ITEMS], F32, 32), on("values6", [P, ITEMS], F32, 40)]
         banks = [psum.tile([P, ITEMS], F32, name=f"bank{t}") for t in range(D_TILES)]
 
         def rows(t):
@@ -76,143 +80,124 @@ def tile_attend_gqr_ab_kernel(tc, aT, bT, W, dz, offs, joffs, out_0, out_1):
         def part_of(entries, h):
             return entries[:, h * HALF // LIST_STRIPE : (h + 1) * HALF // LIST_STRIPE]
 
-        def cast(copy, grouped, raw, first, last):
-            interleave(copy, grouped[:, PACK * first : PACK * last], raw[:, :, first:last])
+        def cast(copy, grouped, raw, first, last, base=0):
+            interleave(copy, grouped[:, PACK * (first - base) : PACK * (last - base)], raw[:, :, first:last])
 
-        def quantize_dz(h):
+        def quantize_w(first, last, grouped):
             nc.vector.quantize_mx(
-                out=dz_codes[:, half(h)].bitcast(E5M2X4), scales=dz_scales[:, half(h)], in_=dz_bf[h][:]
+                out=w_codes[:, first:last].bitcast(E4M3X4), scales=w_scales[:, first:last], in_=grouped[:]
             )
 
-        def quantize_w(h):
-            nc.vector.quantize_mx(out=w_codes[h][:].bitcast(E4M3X4), scales=w_scales[h][:], in_=w_bf[h][:])
+        def bank_of(t, h):
+            return banks[(t + h - 1) % D_TILES][:, half(1 - h)]
 
-        def multiply(out, t, items):
-            cols = rows(t % 2)
+        def multiply(t, h):
             nc.tensor.matmul_mx(
-                out=out,
-                lhsT=w_codes[t // 2][:, cols].bitcast(E4M3X4),
-                lhsT_scale=w_scales[t // 2][:, cols],
-                rhs=dz_codes[:, items].bitcast(E5M2X4),
-                rhs_scale=dz_scales[:, items],
+                out=bank_of(t, h),
+                lhsT=w_codes[:, rows(t)].bitcast(E4M3X4),
+                lhsT_scale=w_scales[:, rows(t)],
+                rhs=dz_codes[:, half(h)].bitcast(E5M2X4),
+                rhs_scale=dz_scales[:, half(h)],
                 start=True,
                 stop=True,
             )
 
-        def multiply_half(t, h):
-            multiply(banks[(t + h - 1) % 3][:, half(1 - h)], t, half(h))
-
-        def load_a(t):
-            nc.sync.dma_start(out=a_tab[t][:], in_=aT[rows(t), :])
-
-        def load_b(t):
-            nc.sync.dma_start(out=b_tab[t][:], in_=bT[rows(t), :])
-
-        def load_w(h):
-            nc.sync.dma_start(out=w_raw[h][:], in_=W.rearrange("(p t) d -> p t d", t=PACK)[:, :, half(h)])
-
-        def load_dz(h):
-            nc.sync.dma_start(out=dz_raw[h][:], in_=dz.rearrange("(p t) i -> p t i", t=PACK)[:, :, half(h)])
-
-        tabs = b_tab[0:3] + a_tab[0:3]
-        gather_lists = [b_list] * 3 + [a_list] * 3
-        scatter_lists = [a_list] * 3 + [b_list] * 3
-        wins = win_0[0:3] + win_1[0:3]
-        outs = [out_0] * 3 + [out_1] * 3
+        tabs = b_tab + a_tab[0:2]
+        gather_lists = [b_list] * 4 + [a_list] * 2
+        scatter_lists = [a_list] * 4 + [b_list] * 2
+        wins = win_0 + win_1[0:2]
+        outs = [out_0] * 4 + [out_1] * 2
 
         def gather(k):
-            nc.vector.tensor_copy(got[:, k * ITEMS : (k + 1) * ITEMS], tabs[k][:].indirect(gather_lists[k][:]))
+            nc.vector.tensor_copy(got[:, k * ITEMS : (k + 1) * ITEMS], tabs[k].indirect(gather_lists[k][:]))
 
         def gather_half(k, h):
             at = k * ITEMS + h * HALF
-            nc.vector.tensor_copy(got[:, at : at + HALF], tabs[k][:].indirect(part_of(gather_lists[k], h)))
-
-        def product(k):
-            first = HALF if k == 0 else 0
-            last = HALF if k == UNITS else ITEMS
-            at = k * ITEMS - HALF
-            nc.vector.tensor_tensor(
-                values[k][:, first:last], banks[(k - 1) % 3][:, first:last], got[:, at + first : at + last], MULT
-            )
+            nc.vector.tensor_copy(got[:, at : at + HALF], tabs[k].indirect(part_of(gather_lists[k], h)))
 
         def scatter(k, h):
             nc.scalar.activation(
                 wins[k][:].indirect(part_of(scatter_lists[k], h)), values[k + h][:, half(1 - h)], COPY
             )
 
-        def step(k, made=False):
-            if not made:
-                product(k)
+        def product(k):
+            first = HALF if k == 0 else 0
+            last = HALF if k == UNITS else ITEMS
+            at = k * ITEMS - HALF
+            nc.vector.tensor_tensor(
+                values[k][:, first:last], banks[(k - 1) % D_TILES][:, first:last], got[:, at + first : at + last], MULT
+            )
+
+        def put(k):
             if k < UNITS:
                 scatter(k, 0)
             if k > 0:
                 scatter(k - 1, 1)
-                nc.sync.dma_start(out=outs[k - 1][rows((k - 1) % 3), :], in_=wins[k - 1][:])
+                nc.sync.dma_start(out=outs[k - 1][rows((k - 1) % D_TILES), :], in_=wins[k - 1][:])
 
-        def put_v(out, window, entries, gathered):
-            nc.vector.tensor_tensor(window[:].indirect(entries[:]), de_3[:], gathered[:], MULT)
-            nc.sync.dma_start(out=out[rows(3), :], in_=window[:])
+        def step(k):
+            product(k)
+            put(k)
 
         def clear(window):
             nc.gpsimd.memset(window[:].bitcast(I32), 0)
 
-        load_dz(0)
+        nc.sync.dma_start(out=dz_raw[:], in_=dz.rearrange("(p t) i -> p t i", t=PACK))
+        nc.sync.dma_start(out=w_raw[:], in_=W.rearrange("(p t) d -> p t d", t=PACK))
         nc.sync.dma_start(b_list[:], joffs)
-        load_b(0)
-        load_w(0)
+        nc.sync.dma_start(out=b_tab[0], in_=bT[rows(0), :])
         nc.sync.dma_start(a_list[:], offs)
-        load_dz(1)
-        load_b(1)
-        load_w(1)
-        load_b(2)
-        load_a(0)
-        load_a(1)
-        load_b(3)
-        load_a(2)
-        load_a(3)
+        nc.sync.dma_start(out=b_tab[1], in_=bT[rows(1), :])
+        nc.sync.dma_start(
+            out=b_pair[:].rearrange("p (t c) -> p t c", t=2), in_=bT[PAIR:D, :].rearrange("(t p) c -> p t c", t=2)
+        )
+        nc.sync.dma_start(
+            out=a_pair[:].rearrange("p (t c) -> p t c", t=2), in_=aT[0:PAIR, :].rearrange("(t p) c -> p t c", t=2)
+        )
+        for t in (2, 3):
+            nc.sync.dma_start(out=a_tab[t], in_=aT[rows(t), :])
 
-        for window in win_0[0:3]:
+        for window in win_0[0:2]:
             nc.vector.memset(window[:].bitcast(I32), 0)
 
-        cast(nc.scalar.copy, dz_bf[0], dz_raw[0], 0, HALF)
-        nc.scalar.activation(got[:, 0:ITEMS], b_tab[0][:].indirect(b_list[:]), COPY)
-        quantize_dz(0)
-        cast(nc.vector.tensor_copy, w_bf[0], w_raw[0], 0, 192)
-        cast(nc.scalar.copy, w_bf[0], w_raw[0], 192, PAIR)
-        quantize_w(0)
-        multiply_half(0, 0)
-        multiply_half(1, 0)
-        cast(nc.vector.tensor_copy, dz_bf[1], dz_raw[1], 0, 160)
-        cast(nc.scalar.copy, dz_bf[1], dz_raw[1], 160, HALF)
+        cast(nc.scalar.copy, dz_bf, dz_raw, 0, 192)
+        cast(nc.vector.tensor_copy, dz_bf, dz_raw, 192, ITEMS)
+        nc.vector.quantize_mx(out=dz_codes[:].bitcast(E5M2X4), scales=dz_scales[:], in_=dz_bf[:])
+        cast(nc.vector.tensor_copy, w_bf[0], w_raw, 0, PAIR)
+        cast(nc.scalar.copy, w_bf[1], w_raw, PAIR, D, base=PAIR)
+        quantize_w(0, PAIR, w_bf[0])
+        for t in (0, 1):
+            multiply(t, 0)
+            multiply(t, 1)
+        gather_half(0, 0)
+        nc.scalar.activation(got[:, half(1)], b_tab[0].indirect(part_of(b_list, 1)), COPY)
+        quantize_w(PAIR, D, w_bf[1])
         step(0)
-        quantize_dz(1)
-        multiply_half(0, 1)
-        multiply_half(1, 1)
+        clear(win_0[2])
+        clear(win_0[3])
+        for t in (2, 3):
+            multiply(t, 0)
+            multiply(t, 1)
         gather_half(1, 0)
         step(1)
-        cast(nc.vector.tensor_copy, w_bf[1], w_raw[1], 0, PAIR)
-        gather_half(1, 1)
-        quantize_w(1)
         clear(win_1[0])
-        clear(win_0[3])
-        multiply_half(2, 0)
-        multiply_half(2, 1)
-        multiply(banks[3][:], 3, slice(0, ITEMS))
-        gather(2)
-        step(2)
-        nc.scalar.copy(out=de_3[:], in_=banks[3][:])
         clear(win_1[1])
-        clear(win_1[2])
+        gather_half(1, 1)
+        gather(2)
         gather(3)
-        step(3)
+        step(2)
+        clear(win_1[2])
         clear(win_1[3])
+        step(3)
+        for t in (2, 3):
+            for h in range(2):
+                nc.vector.tensor_copy(de[t][:, half(h)], bank_of(t, h))
         gather(4)
-        step(4)
         gather(5)
-        nc.vector.tensor_copy(got_3[0][:], b_tab[3][:].indirect(b_list[:]))
-        product(5)
-        put_v(out_0, win_0[3], a_list, got_3[0])
-        step(5, made=True)
-        step(6)
-        nc.vector.tensor_copy(got_3[1][:], a_tab[3][:].indirect(a_list[:]))
-        put_v(out_1, win_1[3], b_list, got_3[1])
+        step(4)
+        for t in (2, 3):
+            nc.vector.tensor_copy(got_v[t][:], a_tab[t].indirect(a_list[:]))
+            product(t + 3)
+            nc.vector.tensor_tensor(win_1[t][:].indirect(b_list[:]), de[t][:], got_v[t][:], MULT)
+            nc.sync.dma_start(out=out_1[rows(t), :], in_=win_1[t][:])
+            put(t + 3)

@@ -46,18 +46,17 @@ def tile_attend_gqr_ab_kernel(tc, aT, bT, W, dz, offs, joffs, out_0, out_1):
         a_list = keep.tile([P, ITEMS // LIST_STRIPE], U16, name="a_list")
         b_list = keep.tile([P, ITEMS // LIST_STRIPE], U16, name="b_list")
         dz_raw = keep.tile([P, PACK, ITEMS], F32, name="dz_raw")
-        w_raw = keep.tile([P, PACK, D], F32, name="w_raw")
+        w_raw = [keep.tile([P, PACK, PAIR], F32, name=f"w_raw{h}") for h in range(2)]
         a_pair = keep.tile([P, 2 * A_COLS], F32, name="a_pair")
         a_tab = [a_pair[:, 0:A_COLS], a_pair[:, A_COLS:]]
         a_tab = a_tab + [on(f"a_tab{t}", [P, A_COLS], F32, 16 + 8 * t)[:] for t in (2, 3)]
-        b_pair = on("b_pair", [P, 2 * B_COLS], F32, 24)
-        b_tab = [keep.tile([P, B_COLS], F32, name=f"b_tab{t}")[:] for t in range(2)]
-        b_tab = b_tab + [b_pair[:, 0:B_COLS], b_pair[:, B_COLS:]]
+        b_tab = [keep.tile([P, B_COLS], F32, name=f"b_tab{t}")[:] for t in range(3)]
+        b_tab.append(on("b_tab3", [P, B_COLS], F32, 24)[:])
         win_0 = [keep.tile([P, A_COLS], F32, name=f"win_0_{t}") for t in range(2)]
-        win_0 = win_0 + [on("win_0_2", [P, A_COLS], F32, 48), on("win_0_3", [P, A_COLS], F32, 56)]
+        win_0 = win_0 + [on("win_0_2", [P, A_COLS], F32, 48), on("win_0_3", [P, A_COLS], F32, 0)]
         win_1 = [on(f"win_1_{t}", [P, B_COLS], F32, 8 + 4 * t) for t in range(D_TILES)]
         dz_bf = keep.tile([P, ITEMS * PACK], BF16, name="dz_bf", align_bytes=64)
-        w_bf = [keep.tile([P, PAIR * PACK], BF16, name="w_bf0", align_bytes=64), on("w_bf1", [P, PAIR * PACK], BF16, 55)]
+        w_bf = [on("w_bf0", [P, PAIR * PACK], BF16, 48), on("w_bf1", [P, PAIR * PACK], BF16, 7)]
         dz_codes = keep.tile([P, ITEMS], U32, name="dz_codes", align_bytes=64)
         dz_scales = keep.tile([P, ITEMS], U8, name="dz_scales", align_bytes=64)
         w_codes = keep.tile([P, D], U32, name="w_codes", align_bytes=64)
@@ -65,9 +64,9 @@ def tile_attend_gqr_ab_kernel(tc, aT, bT, W, dz, offs, joffs, out_0, out_1):
         de = {2: on("de2", [P, ITEMS], F32, 24), 3: on("de3", [P, ITEMS], F32, 26)}
         got = keep.tile([P, UNITS * ITEMS], F32, name="got")
         got_v = {t: keep.tile([P, ITEMS], F32, name=f"got_v{t}") for t in (2, 3)}
-        values = [keep.tile([P, ITEMS], F32, name="values0")]
-        values = values + [on("values1", [P, ITEMS], F32, 11), on("values2", [P, ITEMS], F32, 19)]
-        values = values + [keep.tile([P, ITEMS], F32, name=f"values{k}") for k in (3, 4)]
+        values = [keep.tile([P, ITEMS], F32, name=f"values{k}") for k in range(2)]
+        values = values + [on("values2", [P, ITEMS], F32, 15), on("values3", [P, ITEMS], F32, 20)]
+        values = values + [keep.tile([P, ITEMS], F32, name="values4")]
         values = values + [on("values5", [P, ITEMS], F32, 32), on("values6", [P, ITEMS], F32, 40)]
         banks = [psum.tile([P, ITEMS], F32, name=f"bank{t}") for t in range(D_TILES)]
 
@@ -143,14 +142,15 @@ def tile_attend_gqr_ab_kernel(tc, aT, bT, W, dz, offs, joffs, out_0, out_1):
             nc.gpsimd.memset(window[:].bitcast(I32), 0)
 
         nc.sync.dma_start(out=dz_raw[:], in_=dz.rearrange("(p t) i -> p t i", t=PACK))
-        nc.sync.dma_start(out=w_raw[:], in_=W.rearrange("(p t) d -> p t d", t=PACK))
+        w_rows = W.rearrange("(p t) d -> p t d", t=PACK)
+        nc.sync.dma_start(out=w_raw[0][:], in_=w_rows[:, :, 0:PAIR])
         nc.sync.dma_start(b_list[:], joffs)
         nc.sync.dma_start(out=b_tab[0], in_=bT[rows(0), :])
         nc.sync.dma_start(a_list[:], offs)
         nc.sync.dma_start(out=b_tab[1], in_=bT[rows(1), :])
-        nc.sync.dma_start(
-            out=b_pair[:].rearrange("p (t c) -> p t c", t=2), in_=bT[PAIR:D, :].rearrange("(t p) c -> p t c", t=2)
-        )
+        nc.sync.dma_start(out=w_raw[1][:], in_=w_rows[:, :, PAIR:D])
+        for t in (2, 3):
+            nc.sync.dma_start(out=b_tab[t], in_=bT[rows(t), :])
         nc.sync.dma_start(
             out=a_pair[:].rearrange("p (t c) -> p t c", t=2), in_=aT[0:PAIR, :].rearrange("(t p) c -> p t c", t=2)
         )
@@ -162,39 +162,41 @@ def tile_attend_gqr_ab_kernel(tc, aT, bT, W, dz, offs, joffs, out_0, out_1):
 
         cast(nc.scalar.copy, dz_bf, dz_raw, 0, 192)
         cast(nc.vector.tensor_copy, dz_bf, dz_raw, 192, ITEMS)
+        cast(nc.vector.tensor_copy, w_bf[0], w_raw[0], 0, 160)
+        cast(nc.scalar.copy, w_bf[0], w_raw[0], 160, PAIR)
         nc.vector.quantize_mx(out=dz_codes[:].bitcast(E5M2X4), scales=dz_scales[:], in_=dz_bf[:])
-        cast(nc.vector.tensor_copy, w_bf[0], w_raw, 0, PAIR)
-        cast(nc.scalar.copy, w_bf[1], w_raw, PAIR, D, base=PAIR)
         quantize_w(0, PAIR, w_bf[0])
+        clear(win_0[2])
         for t in (0, 1):
             multiply(t, 0)
             multiply(t, 1)
         gather_half(0, 0)
         nc.scalar.activation(got[:, half(1)], b_tab[0].indirect(part_of(b_list, 1)), COPY)
-        quantize_w(PAIR, D, w_bf[1])
         step(0)
-        clear(win_0[2])
+        gather_half(1, 0)
+        step(1)
+        cast(nc.vector.tensor_copy, w_bf[1], w_raw[1], 0, PAIR)
+        gather_half(1, 1)
+        quantize_w(PAIR, D, w_bf[1])
         clear(win_0[3])
+        clear(win_1[0])
         for t in (2, 3):
             multiply(t, 0)
             multiply(t, 1)
-        gather_half(1, 0)
-        step(1)
-        clear(win_1[0])
-        clear(win_1[1])
-        gather_half(1, 1)
         gather(2)
-        gather(3)
         step(2)
+        clear(win_1[1])
         clear(win_1[2])
-        clear(win_1[3])
+        gather(3)
         step(3)
-        for t in (2, 3):
-            for h in range(2):
-                nc.vector.tensor_copy(de[t][:, half(h)], bank_of(t, h))
+        clear(win_1[3])
+        for h in range(2):
+            nc.vector.tensor_copy(de[2][:, half(h)], bank_of(2, h))
         gather(4)
         gather(5)
         step(4)
+        for h in range(2):
+            nc.scalar.copy(out=de[3][:, half(h)], in_=bank_of(3, h))
         for t in (2, 3):
             nc.vector.tensor_copy(got_v[t][:], a_tab[t].indirect(a_list[:]))
             product(t + 3)

@@ -47,11 +47,9 @@ def tile_attend_gqr_ab_kernel(tc, aT, bT, W, dz, offs, joffs, out_0, out_1):
         b_list = keep.tile([P, ITEMS // LIST_STRIPE], U16, name="b_list")
         dz_raw = keep.tile([P, PACK, ITEMS], F32, name="dz_raw")
         w_raw = [keep.tile([P, PACK, PAIR], F32, name=f"w_raw{h}") for h in range(2)]
-        a_pair = keep.tile([P, 2 * A_COLS], F32, name="a_pair")
-        a_tab = [a_pair[:, 0:A_COLS], a_pair[:, A_COLS:]]
+        a_tab = [keep.tile([P, A_COLS], F32, name=f"a_tab{t}")[:] for t in range(2)]
         a_tab = a_tab + [on(f"a_tab{t}", [P, A_COLS], F32, 16 + 8 * t)[:] for t in (2, 3)]
-        b_tab = [keep.tile([P, B_COLS], F32, name=f"b_tab{t}")[:] for t in range(3)]
-        b_tab.append(on("b_tab3", [P, B_COLS], F32, 24)[:])
+        b_tab = [keep.tile([P, B_COLS], F32, name=f"b_tab{t}")[:] for t in range(D_TILES)]
         win_0 = [keep.tile([P, A_COLS], F32, name=f"win_0_{t}") for t in range(2)]
         win_0 = win_0 + [on("win_0_2", [P, A_COLS], F32, 48), on("win_0_3", [P, A_COLS], F32, 0)]
         win_1 = [on(f"win_1_{t}", [P, B_COLS], F32, 8 + 4 * t) for t in range(D_TILES)]
@@ -61,7 +59,8 @@ def tile_attend_gqr_ab_kernel(tc, aT, bT, W, dz, offs, joffs, out_0, out_1):
         dz_scales = keep.tile([P, ITEMS], U8, name="dz_scales", align_bytes=64)
         w_codes = keep.tile([P, D], U32, name="w_codes", align_bytes=64)
         w_scales = keep.tile([P, D], U8, name="w_scales", align_bytes=64)
-        de = {2: on("de2", [P, ITEMS], F32, 24), 3: on("de3", [P, ITEMS], F32, 26)}
+        de_late = keep.tile([P, 2 * ITEMS], F32, name="de_late")
+        de = {2: de_late[:, 0:ITEMS], 3: de_late[:, ITEMS:]}
         got = keep.tile([P, UNITS * ITEMS], F32, name="got")
         got_v = {t: keep.tile([P, ITEMS], F32, name=f"got_v{t}") for t in (2, 3)}
         values = [keep.tile([P, ITEMS], F32, name=f"values{k}") for k in range(2)]
@@ -151,10 +150,7 @@ def tile_attend_gqr_ab_kernel(tc, aT, bT, W, dz, offs, joffs, out_0, out_1):
         nc.sync.dma_start(out=w_raw[1][:], in_=w_rows[:, :, PAIR:D])
         for t in (2, 3):
             nc.sync.dma_start(out=b_tab[t], in_=bT[rows(t), :])
-        nc.sync.dma_start(
-            out=a_pair[:].rearrange("p (t c) -> p t c", t=2), in_=aT[0:PAIR, :].rearrange("(t p) c -> p t c", t=2)
-        )
-        for t in (2, 3):
+        for t in range(D_TILES):
             nc.sync.dma_start(out=a_tab[t], in_=aT[rows(t), :])
 
         for window in win_0[0:2]:
@@ -170,13 +166,13 @@ def tile_attend_gqr_ab_kernel(tc, aT, bT, W, dz, offs, joffs, out_0, out_1):
         for t in (0, 1):
             multiply(t, 0)
             multiply(t, 1)
-        gather_half(0, 0)
-        nc.scalar.activation(got[:, half(1)], b_tab[0].indirect(part_of(b_list, 1)), COPY)
+        for h in range(2):
+            nc.scalar.activation(got[:, half(h)], b_tab[0].indirect(part_of(b_list, h)), COPY)
         step(0)
         gather_half(1, 0)
+        gather_half(1, 1)
         step(1)
         cast(nc.vector.tensor_copy, w_bf[1], w_raw[1], 0, PAIR)
-        gather_half(1, 1)
         quantize_w(PAIR, D, w_bf[1])
         clear(win_0[3])
         clear(win_1[0])
@@ -190,16 +186,15 @@ def tile_attend_gqr_ab_kernel(tc, aT, bT, W, dz, offs, joffs, out_0, out_1):
         gather(3)
         step(3)
         clear(win_1[3])
-        for h in range(2):
-            nc.vector.tensor_copy(de[2][:, half(h)], bank_of(2, h))
+        nc.vector.tensor_copy(de_late[:, 0:HALF], bank_of(2, 0))
+        nc.vector.tensor_copy(de_late[:, HALF : HALF + ITEMS], banks[2][:])
+        nc.vector.tensor_copy(de_late[:, HALF + ITEMS :], bank_of(3, 1))
         gather(4)
-        gather(5)
         step(4)
-        for h in range(2):
-            nc.scalar.copy(out=de[3][:, half(h)], in_=bank_of(3, h))
+        gather(5)
         for t in (2, 3):
             nc.vector.tensor_copy(got_v[t][:], a_tab[t].indirect(a_list[:]))
             product(t + 3)
-            nc.vector.tensor_tensor(win_1[t][:].indirect(b_list[:]), de[t][:], got_v[t][:], MULT)
+            nc.vector.tensor_tensor(win_1[t][:].indirect(b_list[:]), de[t], got_v[t][:], MULT)
             nc.sync.dma_start(out=out_1[rows(t), :], in_=win_1[t][:])
             put(t + 3)

@@ -42,31 +42,32 @@ def tile_attend_gqr_ab_kernel(tc, aT, bT, W, dz, offs, joffs, out_0, out_1):
         def on(name, shape, dtype, kib):
             return shared.tile(shape, dtype, name=name, align_bytes=64, offset=kib * KIB)
 
-        UNITS = 6
+        UNITS = 5
         a_list = keep.tile([P, ITEMS // LIST_STRIPE], U16, name="a_list")
         b_list = keep.tile([P, ITEMS // LIST_STRIPE], U16, name="b_list")
         dz_raw = keep.tile([P, PACK, ITEMS], F32, name="dz_raw")
         w_raw = [keep.tile([P, PACK, PAIR], F32, name=f"w_raw{h}") for h in range(2)]
-        a_tab = [keep.tile([P, A_COLS], F32, name=f"a_tab{t}")[:] for t in range(2)]
-        a_tab = a_tab + [on(f"a_tab{t}", [P, A_COLS], F32, 16 + 8 * t)[:] for t in (2, 3)]
-        b_tab = [keep.tile([P, B_COLS], F32, name=f"b_tab{t}")[:] for t in range(D_TILES)]
+        a_pair = keep.tile([P, 2 * A_COLS], F32, name="a_pair")
+        a_tab = [on("a_tab0", [P, A_COLS], F32, 40), a_pair[:, 0:A_COLS], a_pair[:, A_COLS:]]
+        a_tab.append(on("a_tab3", [P, A_COLS], F32, 24))
+        b_pair = keep.tile([P, 2 * B_COLS], F32, name="b_pair")
+        b_tab = [keep.tile([P, B_COLS], F32, name=f"b_tab{t}")[:] for t in range(2)]
+        b_tab = b_tab + [b_pair[:, 0:B_COLS], b_pair[:, B_COLS:]]
         win_0 = [keep.tile([P, A_COLS], F32, name=f"win_0_{t}") for t in range(2)]
         win_0 = win_0 + [on("win_0_2", [P, A_COLS], F32, 48), on("win_0_3", [P, A_COLS], F32, 0)]
-        win_1 = [on(f"win_1_{t}", [P, B_COLS], F32, 8 + 4 * t) for t in range(D_TILES)]
+        win_1 = [on(f"win_1_{t}", [P, B_COLS], F32, at) for t, at in enumerate((8, 12, 24, 16))]
         dz_bf = keep.tile([P, ITEMS * PACK], BF16, name="dz_bf", align_bytes=64)
         w_bf = [on("w_bf0", [P, PAIR * PACK], BF16, 48), on("w_bf1", [P, PAIR * PACK], BF16, 7)]
         dz_codes = keep.tile([P, ITEMS], U32, name="dz_codes", align_bytes=64)
         dz_scales = keep.tile([P, ITEMS], U8, name="dz_scales", align_bytes=64)
         w_codes = keep.tile([P, D], U32, name="w_codes", align_bytes=64)
         w_scales = keep.tile([P, D], U8, name="w_scales", align_bytes=64)
-        de_late = keep.tile([P, 2 * ITEMS], F32, name="de_late")
-        de = {2: de_late[:, 0:ITEMS], 3: de_late[:, ITEMS:]}
+        de = {2: keep.tile([P, ITEMS], F32, name="de2"), 3: on("de3", [P, ITEMS], F32, 40)}
         got = keep.tile([P, UNITS * ITEMS], F32, name="got")
-        got_v = {t: keep.tile([P, ITEMS], F32, name=f"got_v{t}") for t in (2, 3)}
+        got_v = [keep.tile([P, ITEMS], F32, name=f"got_v{k}") for k in range(3)]
         values = [keep.tile([P, ITEMS], F32, name=f"values{k}") for k in range(2)]
-        values = values + [on("values2", [P, ITEMS], F32, 15), on("values3", [P, ITEMS], F32, 20)]
-        values = values + [keep.tile([P, ITEMS], F32, name="values4")]
-        values = values + [on("values5", [P, ITEMS], F32, 32), on("values6", [P, ITEMS], F32, 40)]
+        values = values + [on("values2", [P, ITEMS], F32, 15)]
+        values = values + [keep.tile([P, ITEMS], F32, name=f"values{k}") for k in range(3, UNITS + 1)]
         banks = [psum.tile([P, ITEMS], F32, name=f"bank{t}") for t in range(D_TILES)]
 
         def rows(t):
@@ -78,33 +79,36 @@ def tile_attend_gqr_ab_kernel(tc, aT, bT, W, dz, offs, joffs, out_0, out_1):
         def part_of(entries, h):
             return entries[:, h * HALF // LIST_STRIPE : (h + 1) * HALF // LIST_STRIPE]
 
-        def cast(copy, grouped, raw, first, last, base=0):
-            interleave(copy, grouped[:, PACK * (first - base) : PACK * (last - base)], raw[:, :, first:last])
+        def cast(copy, grouped, raw, first, last):
+            interleave(copy, grouped[:, PACK * first : PACK * last], raw[:, :, first:last])
 
-        def quantize_w(first, last, grouped):
+        def quantize_w(h):
             nc.vector.quantize_mx(
-                out=w_codes[:, first:last].bitcast(E4M3X4), scales=w_scales[:, first:last], in_=grouped[:]
+                out=w_codes[:, half(h)].bitcast(E4M3X4), scales=w_scales[:, half(h)], in_=w_bf[h][:]
             )
 
         def bank_of(t, h):
-            return banks[(t + h - 1) % D_TILES][:, half(1 - h)]
+            return banks[(t + h - 1) % 3][:, half(1 - h)]
 
-        def multiply(t, h):
+        def multiply(out, t, items):
             nc.tensor.matmul_mx(
-                out=bank_of(t, h),
+                out=out,
                 lhsT=w_codes[:, rows(t)].bitcast(E4M3X4),
                 lhsT_scale=w_scales[:, rows(t)],
-                rhs=dz_codes[:, half(h)].bitcast(E5M2X4),
-                rhs_scale=dz_scales[:, half(h)],
+                rhs=dz_codes[:, items].bitcast(E5M2X4),
+                rhs_scale=dz_scales[:, items],
                 start=True,
                 stop=True,
             )
 
-        tabs = b_tab + a_tab[0:2]
-        gather_lists = [b_list] * 4 + [a_list] * 2
-        scatter_lists = [a_list] * 4 + [b_list] * 2
-        wins = win_0 + win_1[0:2]
-        outs = [out_0] * 4 + [out_1] * 2
+        def multiply_halves(t):
+            for h in range(2):
+                multiply(bank_of(t, h), t, half(h))
+
+        tabs = b_tab[0:3] + [a_tab[0][:], a_tab[1]]
+        gather_lists = [b_list] * 3 + [a_list] * 2
+        scatter_lists = [a_list] * 3 + [b_list] * 2
+        wins = win_0[0:3] + win_1[0:2]
 
         def gather(k):
             nc.vector.tensor_copy(got[:, k * ITEMS : (k + 1) * ITEMS], tabs[k].indirect(gather_lists[k][:]))
@@ -118,40 +122,40 @@ def tile_attend_gqr_ab_kernel(tc, aT, bT, W, dz, offs, joffs, out_0, out_1):
                 wins[k][:].indirect(part_of(scatter_lists[k], h)), values[k + h][:, half(1 - h)], COPY
             )
 
-        def product(k):
+        def step(k):
             first = HALF if k == 0 else 0
             last = HALF if k == UNITS else ITEMS
             at = k * ITEMS - HALF
             nc.vector.tensor_tensor(
-                values[k][:, first:last], banks[(k - 1) % D_TILES][:, first:last], got[:, at + first : at + last], MULT
+                values[k][:, first:last], banks[(k - 1) % 3][:, first:last], got[:, at + first : at + last], MULT
             )
-
-        def put(k):
             if k < UNITS:
                 scatter(k, 0)
             if k > 0:
                 scatter(k - 1, 1)
-                nc.sync.dma_start(out=outs[k - 1][rows((k - 1) % D_TILES), :], in_=wins[k - 1][:])
 
-        def step(k):
-            product(k)
-            put(k)
+        def store(out, wins_of_out, t):
+            nc.sync.dma_start(out=out[rows(t), :], in_=wins_of_out[t][:])
 
         def clear(window):
             nc.gpsimd.memset(window[:].bitcast(I32), 0)
 
-        nc.sync.dma_start(out=dz_raw[:], in_=dz.rearrange("(p t) i -> p t i", t=PACK))
         w_rows = W.rearrange("(p t) d -> p t d", t=PACK)
-        nc.sync.dma_start(out=w_raw[0][:], in_=w_rows[:, :, 0:PAIR])
+        nc.sync.dma_start(out=dz_raw[:], in_=dz.rearrange("(p t) i -> p t i", t=PACK))
+        nc.sync.dma_start(out=w_raw[0][:], in_=w_rows[:, :, half(0)])
         nc.sync.dma_start(b_list[:], joffs)
         nc.sync.dma_start(out=b_tab[0], in_=bT[rows(0), :])
         nc.sync.dma_start(a_list[:], offs)
         nc.sync.dma_start(out=b_tab[1], in_=bT[rows(1), :])
-        nc.sync.dma_start(out=w_raw[1][:], in_=w_rows[:, :, PAIR:D])
-        for t in (2, 3):
-            nc.sync.dma_start(out=b_tab[t], in_=bT[rows(t), :])
-        for t in range(D_TILES):
-            nc.sync.dma_start(out=a_tab[t], in_=aT[rows(t), :])
+        nc.sync.dma_start(out=w_raw[1][:], in_=w_rows[:, :, half(1)])
+        nc.sync.dma_start(
+            out=b_pair[:].rearrange("p (t c) -> p t c", t=2), in_=bT[PAIR:D, :].rearrange("(t p) c -> p t c", t=2)
+        )
+        nc.sync.dma_start(out=a_tab[0][:], in_=aT[rows(0), :])
+        nc.sync.dma_start(
+            out=a_pair[:].rearrange("p (t c) -> p t c", t=2), in_=aT[P : 3 * P, :].rearrange("(t p) c -> p t c", t=2)
+        )
+        nc.sync.dma_start(out=a_tab[3][:], in_=aT[rows(3), :])
 
         for window in win_0[0:2]:
             nc.vector.memset(window[:].bitcast(I32), 0)
@@ -161,40 +165,44 @@ def tile_attend_gqr_ab_kernel(tc, aT, bT, W, dz, offs, joffs, out_0, out_1):
         cast(nc.vector.tensor_copy, w_bf[0], w_raw[0], 0, 160)
         cast(nc.scalar.copy, w_bf[0], w_raw[0], 160, PAIR)
         nc.vector.quantize_mx(out=dz_codes[:].bitcast(E5M2X4), scales=dz_scales[:], in_=dz_bf[:])
-        quantize_w(0, PAIR, w_bf[0])
+        quantize_w(0)
         clear(win_0[2])
-        for t in (0, 1):
-            multiply(t, 0)
-            multiply(t, 1)
+        multiply_halves(0)
+        multiply_halves(1)
         for h in range(2):
             nc.scalar.activation(got[:, half(h)], b_tab[0].indirect(part_of(b_list, h)), COPY)
         step(0)
         gather_half(1, 0)
         gather_half(1, 1)
         step(1)
+        store(out_0, win_0, 0)
         cast(nc.vector.tensor_copy, w_bf[1], w_raw[1], 0, PAIR)
-        quantize_w(PAIR, D, w_bf[1])
+        quantize_w(1)
         clear(win_0[3])
         clear(win_1[0])
-        for t in (2, 3):
-            multiply(t, 0)
-            multiply(t, 1)
+        multiply_halves(2)
+        multiply(banks[3][:], 3, slice(0, ITEMS))
+        nc.scalar.activation(got_v[0][:], b_tab[3].indirect(b_list[:]), COPY)
         gather(2)
         step(2)
+        store(out_0, win_0, 1)
         clear(win_1[1])
-        clear(win_1[2])
-        gather(3)
-        step(3)
         clear(win_1[3])
-        nc.vector.tensor_copy(de_late[:, 0:HALF], bank_of(2, 0))
-        nc.vector.tensor_copy(de_late[:, HALF : HALF + ITEMS], banks[2][:])
-        nc.vector.tensor_copy(de_late[:, HALF + ITEMS :], bank_of(3, 1))
+        gather(3)
+        nc.vector.tensor_copy(de[3][:], banks[3][:])
+        step(3)
+        nc.scalar.copy(out=de[2][:, half(1)], in_=bank_of(2, 1))
+        nc.vector.tensor_tensor(win_0[3][:].indirect(a_list[:]), de[3][:], got_v[0][:], MULT)
+        store(out_0, win_0, 3)
+        store(out_0, win_0, 2)
+        nc.scalar.activation(got_v[1][:], a_tab[2].indirect(a_list[:]), COPY)
         gather(4)
         step(4)
-        gather(5)
-        for t in (2, 3):
-            nc.vector.tensor_copy(got_v[t][:], a_tab[t].indirect(a_list[:]))
-            product(t + 3)
-            nc.vector.tensor_tensor(win_1[t][:].indirect(b_list[:]), de[t], got_v[t][:], MULT)
-            nc.sync.dma_start(out=out_1[rows(t), :], in_=win_1[t][:])
-            put(t + 3)
+        step(5)
+        nc.vector.tensor_copy(got_v[2][:], a_tab[3][:].indirect(a_list[:]))
+        nc.vector.tensor_copy(de[2][:, half(0)], bank_of(2, 0))
+        clear(win_1[2])
+        nc.vector.tensor_tensor(win_1[3][:].indirect(b_list[:]), de[3][:], got_v[2][:], MULT)
+        nc.vector.tensor_tensor(win_1[2][:].indirect(b_list[:]), de[2][:], got_v[1][:], MULT)
+        for t in (3, 0, 1, 2):
+            store(out_1, win_1, t)

@@ -134,8 +134,8 @@ def tile_attend_gqr_ab_kernel(tc, aT, bT, W, dz, offs, joffs, out_0, out_1):
             if k > 0:
                 scatter(k - 1, 1)
 
-        def store(out, wins_of_out, t):
-            nc.sync.dma_start(out=out[rows(t), :], in_=wins_of_out[t][:])
+        def store(out, wins_of_out, t, queue=nc.sync):
+            queue.dma_start(out=out[rows(t), :], in_=wins_of_out[t][:])
 
         def clear(window):
             nc.gpsimd.memset(window[:].bitcast(I32), 0)
@@ -185,7 +185,7 @@ def tile_attend_gqr_ab_kernel(tc, aT, bT, W, dz, offs, joffs, out_0, out_1):
         nc.scalar.activation(got_v[0][:], b_tab[3].indirect(b_list[:]), COPY)
         gather(2)
         step(2)
-        store(out_0, win_0, 1)
+        store(out_0, win_0, 1, nc.gpsimd)
         clear(win_1[1])
         clear(win_1[3])
         gather(3)
@@ -194,7 +194,7 @@ def tile_attend_gqr_ab_kernel(tc, aT, bT, W, dz, offs, joffs, out_0, out_1):
         nc.scalar.copy(out=de[2][:, half(1)], in_=bank_of(2, 1))
         nc.vector.tensor_tensor(win_0[3][:].indirect(a_list[:]), de[3][:], got_v[0][:], MULT)
         store(out_0, win_0, 3)
-        store(out_0, win_0, 2)
+        store(out_0, win_0, 2, nc.gpsimd)
         nc.scalar.activation(got_v[1][:], a_tab[2].indirect(a_list[:]), COPY)
         gather(4)
         step(4)
@@ -204,5 +204,7 @@ def tile_attend_gqr_ab_kernel(tc, aT, bT, W, dz, offs, joffs, out_0, out_1):
         clear(win_1[2])
         nc.vector.tensor_tensor(win_1[3][:].indirect(b_list[:]), de[3][:], got_v[2][:], MULT)
         nc.vector.tensor_tensor(win_1[2][:].indirect(b_list[:]), de[2][:], got_v[1][:], MULT)
-        for t in (3, 0, 1, 2):
-            store(out_1, win_1, t)
+        store(out_1, win_1, 3, nc.gpsimd)
+        store(out_1, win_1, 0)
+        store(out_1, win_1, 1)
+        store(out_1, win_1, 2)

@@ -69,6 +69,7 @@ def tile_attend_gqr_ab_kernel(tc, aT, bT, W, dz, offs, joffs, out_0, out_1):
         values = values + [on("values2", [P, ITEMS], F32, 15)]
         values = values + [keep.tile([P, ITEMS], F32, name=f"values{k}") for k in range(3, UNITS + 1)]
         banks = [psum.tile([P, ITEMS], F32, name=f"bank{t}") for t in range(D_TILES)]
+        bank_2 = psum.tile([P, ITEMS], F32, name="bank_2")
 
         def rows(t):
             return slice(t * P, (t + 1) * P)
@@ -182,6 +183,7 @@ def tile_attend_gqr_ab_kernel(tc, aT, bT, W, dz, offs, joffs, out_0, out_1):
         clear(win_1[0])
         multiply_halves(2)
         multiply(banks[3][:], 3, slice(0, ITEMS))
+        multiply(bank_2[:], 2, slice(0, ITEMS))
         nc.scalar.activation(got_v[0][:], b_tab[3].indirect(b_list[:]), COPY)
         gather(2)
         step(2)
@@ -191,7 +193,7 @@ def tile_attend_gqr_ab_kernel(tc, aT, bT, W, dz, offs, joffs, out_0, out_1):
         gather(3)
         nc.vector.tensor_copy(de[3][:], banks[3][:])
         step(3)
-        nc.scalar.copy(out=de[2][:, half(1)], in_=bank_of(2, 1))
+        nc.scalar.copy(out=de[2][:], in_=bank_2[:])
         nc.vector.tensor_tensor(win_0[3][:].indirect(a_list[:]), de[3][:], got_v[0][:], MULT)
         store(out_0, win_0, 3)
         store(out_0, win_0, 2, nc.gpsimd)
@@ -200,7 +202,6 @@ def tile_attend_gqr_ab_kernel(tc, aT, bT, W, dz, offs, joffs, out_0, out_1):
         step(4)
         step(5)
         nc.vector.tensor_copy(got_v[2][:], a_tab[3][:].indirect(a_list[:]))
-        nc.vector.tensor_copy(de[2][:, half(0)], bank_of(2, 0))
         clear(win_1[2])
         nc.vector.tensor_tensor(win_1[3][:].indirect(b_list[:]), de[3][:], got_v[2][:], MULT)
         nc.vector.tensor_tensor(win_1[2][:].indirect(b_list[:]), de[2][:], got_v[1][:], MULT)

@@ -23,6 +23,7 @@ HALF = ITEMS // 2
 PAIR = 2 * P
 LIST_STRIPE = 16
 KIB = 1024
+SPLIT = 352
 
 
 def interleave(copy, grouped, raw):
@@ -39,37 +40,40 @@ def tile_attend_gqr_ab_kernel(tc, aT, bT, W, dz, offs, joffs, out_0, out_1):
         shared = ctx.enter_context(tc.tile_pool(name="shared", bufs=1))
         psum = ctx.enter_context(tc.psum_pool(name="psum", bufs=1))
 
-        def on(name, shape, dtype, kib):
-            return shared.tile(shape, dtype, name=name, align_bytes=64, offset=kib * KIB)
+        def on(name, shape, dtype, at):
+            return shared.tile(shape, dtype, name=name, align_bytes=64, offset=at)
 
-        UNITS = 5
         a_list = keep.tile([P, ITEMS // LIST_STRIPE], U16, name="a_list")
         b_list = keep.tile([P, ITEMS // LIST_STRIPE], U16, name="b_list")
         dz_raw = keep.tile([P, PACK, ITEMS], F32, name="dz_raw")
         w_raw = [keep.tile([P, PACK, PAIR], F32, name=f"w_raw{h}") for h in range(2)]
-        a_pair = keep.tile([P, 2 * A_COLS], F32, name="a_pair")
-        a_tab = [on("a_tab0", [P, A_COLS], F32, 40), a_pair[:, 0:A_COLS], a_pair[:, A_COLS:]]
-        a_tab.append(on("a_tab3", [P, A_COLS], F32, 24))
+        a_even = keep.tile([P, 2 * A_COLS], F32, name="a_even")
+        a_odd = keep.tile([P, 2 * A_COLS], F32, name="a_odd")
+        b_0 = keep.tile([P, B_COLS], F32, name="b_0")
+        b_1 = on("b_1", [P, B_COLS], F32, 20 * KIB)
         b_pair = keep.tile([P, 2 * B_COLS], F32, name="b_pair")
-        b_tab = [keep.tile([P, B_COLS], F32, name=f"b_tab{t}")[:] for t in range(2)]
-        b_tab = b_tab + [b_pair[:, 0:B_COLS], b_pair[:, B_COLS:]]
-        win_0 = [keep.tile([P, A_COLS], F32, name=f"win_0_{t}") for t in range(2)]
-        win_0 = win_0 + [on("win_0_2", [P, A_COLS], F32, 48), on("win_0_3", [P, A_COLS], F32, 0)]
-        win_1 = [on(f"win_1_{t}", [P, B_COLS], F32, at) for t, at in enumerate((8, 12, 24, 16))]
+        win_0 = {t: keep.tile([P, A_COLS], F32, name=f"win_0_{t}") for t in (0, 1, 3)}
+        win_0 = [win_0[0], win_0[1], on("win_0_2", [P, A_COLS], F32, 0), win_0[3]]
+        win_1 = [on(f"win_1_{t}", [P, B_COLS], F32, at * KIB) for t, at in enumerate((22, 18, 8, 12))]
         dz_bf = keep.tile([P, ITEMS * PACK], BF16, name="dz_bf", align_bytes=64)
-        w_bf = [on("w_bf0", [P, PAIR * PACK], BF16, 48), on("w_bf1", [P, PAIR * PACK], BF16, 7)]
+        w_bf = [keep.tile([P, PAIR * PACK], BF16, name="w_bf0", align_bytes=64)]
+        w_bf.append(on("w_bf1", [P, PAIR * PACK], BF16, 7 * KIB))
         dz_codes = keep.tile([P, ITEMS], U32, name="dz_codes", align_bytes=64)
         dz_scales = keep.tile([P, ITEMS], U8, name="dz_scales", align_bytes=64)
-        w_codes = keep.tile([P, D], U32, name="w_codes", align_bytes=64)
-        w_scales = keep.tile([P, D], U8, name="w_scales", align_bytes=64)
-        de = {2: keep.tile([P, ITEMS], F32, name="de2"), 3: on("de3", [P, ITEMS], F32, 40)}
-        got = keep.tile([P, UNITS * ITEMS], F32, name="got")
-        got_v = [keep.tile([P, ITEMS], F32, name=f"got_v{k}") for k in range(3)]
-        values = [keep.tile([P, ITEMS], F32, name=f"values{k}") for k in range(2)]
-        values = values + [on("values2", [P, ITEMS], F32, 15)]
-        values = values + [keep.tile([P, ITEMS], F32, name=f"values{k}") for k in range(3, UNITS + 1)]
-        banks = [psum.tile([P, ITEMS], F32, name=f"bank{t}") for t in range(D_TILES)]
-        bank_2 = psum.tile([P, ITEMS], F32, name="bank_2")
+        w_codes = [keep.tile([P, PAIR], U32, name="w_codes0", align_bytes=64)]
+        w_codes.append(on("w_codes1", [P, PAIR], U32, 21 * KIB + KIB // 2))
+        w_scales = [keep.tile([P, PAIR], U8, name="w_scales0", align_bytes=64)]
+        w_scales.append(on("w_scales1", [P, PAIR], U8, 12 * KIB))
+        de = {1: on("de1", [P, ITEMS], F32, 48 * KIB), 3: keep.tile([P, ITEMS], F32, name="de3")}
+        got_first = [keep.tile([P, HALF], F32, name="got_first0"), on("got_first1", [P, HALF], F32, 48 * KIB)]
+        got = keep.tile([P, 5 * HALF], F32, name="got")
+        got_b = {t: keep.tile([P, ITEMS], F32, name=f"got_b{t}") for t in (1, 3)}
+        got_a = {t: keep.tile([P, ITEMS], F32, name=f"got_a{t}") for t in (1, 3)}
+        first = [keep.tile([P, HALF], F32, name=f"first{h}") for h in range(2)]
+        values = [keep.tile([P, HALF], F32, name="values0"), keep.tile([P, ITEMS], F32, name="values1")]
+        values = values + [keep.tile([P, ITEMS], F32, name="values2"), keep.tile([P, HALF], F32, name="values3")]
+        whole = {t: psum.tile([P, ITEMS], F32, name=f"bank{t}") for t in (1, 3)}
+        mixed = [psum.tile([P, ITEMS], F32, name=f"mixed{h}") for h in range(2)]
 
         def rows(t):
             return slice(t * P, (t + 1) * P)
@@ -77,89 +81,70 @@ def tile_attend_gqr_ab_kernel(tc, aT, bT, W, dz, offs, joffs, out_0, out_1):
         def half(h):
             return slice(h * HALF, (h + 1) * HALF)
 
-        def part_of(entries, h):
-            return entries[:, h * HALF // LIST_STRIPE : (h + 1) * HALF // LIST_STRIPE]
+        def part(entries, first_item, last_item):
+            return entries[:, first_item // LIST_STRIPE : last_item // LIST_STRIPE]
 
-        def cast(copy, grouped, raw, first, last):
-            interleave(copy, grouped[:, PACK * first : PACK * last], raw[:, :, first:last])
+        def half_of(entries, h):
+            return part(entries, h * HALF, (h + 1) * HALF)
+
+        def cast(copy, grouped, raw, first_col, last_col):
+            interleave(copy, grouped[:, PACK * first_col : PACK * last_col], raw[:, :, first_col:last_col])
 
         def quantize_w(h):
-            nc.vector.quantize_mx(
-                out=w_codes[:, half(h)].bitcast(E4M3X4), scales=w_scales[:, half(h)], in_=w_bf[h][:]
-            )
-
-        def bank_of(t, h):
-            return banks[(t + h - 1) % 3][:, half(1 - h)]
+            nc.vector.quantize_mx(out=w_codes[h][:].bitcast(E4M3X4), scales=w_scales[h][:], in_=w_bf[h][:])
 
         def multiply(out, t, items):
             nc.tensor.matmul_mx(
                 out=out,
-                lhsT=w_codes[:, rows(t)].bitcast(E4M3X4),
-                lhsT_scale=w_scales[:, rows(t)],
+                lhsT=w_codes[t // 2][:, rows(t % 2)].bitcast(E4M3X4),
+                lhsT_scale=w_scales[t // 2][:, rows(t % 2)],
                 rhs=dz_codes[:, items].bitcast(E5M2X4),
                 rhs_scale=dz_scales[:, items],
                 start=True,
                 stop=True,
             )
 
-        def multiply_halves(t):
-            for h in range(2):
-                multiply(bank_of(t, h), t, half(h))
-
-        tabs = b_tab[0:3] + [a_tab[0][:], a_tab[1]]
-        gather_lists = [b_list] * 3 + [a_list] * 2
-        scatter_lists = [a_list] * 3 + [b_list] * 2
-        wins = win_0[0:3] + win_1[0:2]
-
-        def gather(k):
-            nc.vector.tensor_copy(got[:, k * ITEMS : (k + 1) * ITEMS], tabs[k].indirect(gather_lists[k][:]))
-
-        def gather_half(k, h):
-            at = k * ITEMS + h * HALF
-            nc.vector.tensor_copy(got[:, at : at + HALF], tabs[k].indirect(part_of(gather_lists[k], h)))
-
-        def scatter(k, h):
-            nc.scalar.activation(
-                wins[k][:].indirect(part_of(scatter_lists[k], h)), values[k + h][:, half(1 - h)], COPY
-            )
-
-        def step(k):
-            first = HALF if k == 0 else 0
-            last = HALF if k == UNITS else ITEMS
-            at = k * ITEMS - HALF
-            nc.vector.tensor_tensor(
-                values[k][:, first:last], banks[(k - 1) % 3][:, first:last], got[:, at + first : at + last], MULT
-            )
-            if k < UNITS:
-                scatter(k, 0)
-            if k > 0:
-                scatter(k - 1, 1)
-
-        def store(out, wins_of_out, t, queue=nc.sync):
-            queue.dma_start(out=out[rows(t), :], in_=wins_of_out[t][:])
+        def de_half(t, h):
+            return mixed[(t // 2 + h) % 2][:, half(1 - h)]
 
         def clear(window):
             nc.gpsimd.memset(window[:].bitcast(I32), 0)
+
+        def gather_scalar(out, table, entries):
+            nc.scalar.activation(out, table.indirect(entries), COPY)
+
+        def gather_vector(out, table, entries):
+            nc.vector.tensor_copy(out, table.indirect(entries))
+
+        def product(out, bank, gathered):
+            nc.vector.tensor_tensor(out, bank, gathered, MULT)
+
+        def scatter_half(window, entries, vals, h):
+            nc.scalar.activation(window[:].indirect(half_of(entries, h)), vals, COPY)
+
+        def scatter_product(window, entries, t, gathered):
+            nc.vector.tensor_tensor(window[:].indirect(entries[:]), de[t][:], gathered[:], MULT)
+
+        def store(out, wins, t):
+            nc.sync.dma_start(out=out[rows(t), :], in_=wins[t][:])
 
         w_rows = W.rearrange("(p t) d -> p t d", t=PACK)
         nc.sync.dma_start(out=dz_raw[:], in_=dz.rearrange("(p t) i -> p t i", t=PACK))
         nc.sync.dma_start(out=w_raw[0][:], in_=w_rows[:, :, half(0)])
         nc.sync.dma_start(b_list[:], joffs)
-        nc.sync.dma_start(out=b_tab[0], in_=bT[rows(0), :])
+        nc.sync.dma_start(out=b_0[:], in_=bT[rows(0), :])
         nc.sync.dma_start(a_list[:], offs)
-        nc.sync.dma_start(out=b_tab[1], in_=bT[rows(1), :])
         nc.sync.dma_start(out=w_raw[1][:], in_=w_rows[:, :, half(1)])
+        nc.sync.dma_start(out=b_1[:], in_=bT[rows(1), :])
         nc.sync.dma_start(
             out=b_pair[:].rearrange("p (t c) -> p t c", t=2), in_=bT[PAIR:D, :].rearrange("(t p) c -> p t c", t=2)
         )
-        nc.sync.dma_start(out=a_tab[0][:], in_=aT[rows(0), :])
-        nc.sync.dma_start(
-            out=a_pair[:].rearrange("p (t c) -> p t c", t=2), in_=aT[P : 3 * P, :].rearrange("(t p) c -> p t c", t=2)
-        )
-        nc.sync.dma_start(out=a_tab[3][:], in_=aT[rows(3), :])
+        a_rows = aT.rearrange("(u t p) c -> t p u c", u=2, t=2)
+        for t, pair in enumerate((a_even, a_odd)):
+            nc.sync.dma_start(out=pair[:].rearrange("p (u c) -> p u c", u=2), in_=a_rows[t])
 
-        for window in win_0[0:2]:
-            nc.vector.memset(window[:].bitcast(I32), 0)
+        for t in (0, 1, 3):
+            nc.vector.memset(win_0[t][:].bitcast(I32), 0)
 
         cast(nc.scalar.copy, dz_bf, dz_raw, 0, 192)
         cast(nc.vector.tensor_copy, dz_bf, dz_raw, 192, ITEMS)
@@ -167,45 +152,58 @@ def tile_attend_gqr_ab_kernel(tc, aT, bT, W, dz, offs, joffs, out_0, out_1):
         cast(nc.scalar.copy, w_bf[0], w_raw[0], 160, PAIR)
         nc.vector.quantize_mx(out=dz_codes[:].bitcast(E5M2X4), scales=dz_scales[:], in_=dz_bf[:])
         quantize_w(0)
-        clear(win_0[2])
-        multiply_halves(0)
-        multiply_halves(1)
         for h in range(2):
-            nc.scalar.activation(got[:, half(h)], b_tab[0].indirect(part_of(b_list, h)), COPY)
-        step(0)
-        gather_half(1, 0)
-        gather_half(1, 1)
-        step(1)
+            multiply(de_half(0, h), 0, half(h))
+        multiply(whole[1][:], 1, slice(0, ITEMS))
+
+        gather_scalar(got_first[0][:], b_0[:], half_of(b_list, 0))
+        gather_vector(got_first[1][:], b_0[:], half_of(b_list, 1))
+        for h in range(2):
+            product(first[h][:], de_half(0, h), got_first[h][:])
+        scatter_half(win_0[0], a_list, first[0][:], 0)
+        nc.scalar.copy(out=de[1][:], in_=whole[1][:])
+        scatter_half(win_0[0], a_list, first[1][:], 1)
         store(out_0, win_0, 0)
+
         cast(nc.vector.tensor_copy, w_bf[1], w_raw[1], 0, PAIR)
+        gather_vector(got_b[1][:], b_1[:], b_list[:])
         quantize_w(1)
-        clear(win_0[3])
-        clear(win_1[0])
-        multiply_halves(2)
-        multiply(banks[3][:], 3, slice(0, ITEMS))
-        multiply(bank_2[:], 2, slice(0, ITEMS))
-        nc.scalar.activation(got_v[0][:], b_tab[3].indirect(b_list[:]), COPY)
-        gather(2)
-        step(2)
-        store(out_0, win_0, 1, nc.gpsimd)
-        clear(win_1[1])
-        clear(win_1[3])
-        gather(3)
-        nc.vector.tensor_copy(de[3][:], banks[3][:])
-        step(3)
-        nc.scalar.copy(out=de[2][:], in_=bank_2[:])
-        nc.vector.tensor_tensor(win_0[3][:].indirect(a_list[:]), de[3][:], got_v[0][:], MULT)
+        multiply(whole[3][:], 3, slice(0, ITEMS))
+        for h in range(2):
+            multiply(de_half(2, h), 2, half(h))
+        clear(win_0[2])
+        for t in (1, 0, 2, 3):
+            clear(win_1[t])
+        scatter_product(win_0[1], a_list, 1, got_b[1])
+        store(out_0, win_0, 1)
+
+        nc.scalar.copy(out=de[3][:], in_=whole[3][:])
+        gather_scalar(got[:, 0:ITEMS], b_pair[:, 0:B_COLS], b_list[:])
+        gather_scalar(got_b[3][:, 0:SPLIT], b_pair[:, B_COLS:], part(b_list, 0, SPLIT))
+        gather_vector(got_b[3][:, SPLIT:], b_pair[:, B_COLS:], part(b_list, SPLIT, ITEMS))
+        product(values[0][:], de_half(2, 0), got[:, 0:HALF])
+        scatter_half(win_0[2], a_list, values[0][:], 0)
+        scatter_product(win_0[3], a_list, 3, got_b[3])
         store(out_0, win_0, 3)
-        store(out_0, win_0, 2, nc.gpsimd)
-        nc.scalar.activation(got_v[1][:], a_tab[2].indirect(a_list[:]), COPY)
-        gather(4)
-        step(4)
-        step(5)
-        nc.vector.tensor_copy(got_v[2][:], a_tab[3][:].indirect(a_list[:]))
-        clear(win_1[2])
-        nc.vector.tensor_tensor(win_1[3][:].indirect(b_list[:]), de[3][:], got_v[2][:], MULT)
-        nc.vector.tensor_tensor(win_1[2][:].indirect(b_list[:]), de[2][:], got_v[1][:], MULT)
-        store(out_1, win_1, 3, nc.gpsimd)
+
+        gather_scalar(got[:, ITEMS : 2 * ITEMS], a_even[:, 0:A_COLS], a_list[:])
+        gather_scalar(got[:, 2 * ITEMS :], a_even[:, A_COLS:], half_of(a_list, 0))
+        product(values[1][:], mixed[0][:], got[:, HALF : 3 * HALF])
+        gather_vector(got[:, half(1)], a_even[:, A_COLS:], half_of(a_list, 1))
+        product(values[2][:], mixed[1][:], got[:, 3 * HALF : 5 * HALF])
+        product(values[3][:], de_half(2, 1), got[:, half(1)])
+        scatter_half(win_0[2], a_list, values[1][:, half(0)], 1)
+        store(out_0, win_0, 2)
+        scatter_half(win_1[0], b_list, values[1][:, half(1)], 0)
+        scatter_half(win_1[2], b_list, values[2][:, half(1)], 0)
+        scatter_half(win_1[0], b_list, values[2][:, half(0)], 1)
         store(out_1, win_1, 0)
+
+        gather_vector(got_a[1][:], a_odd[:, 0:A_COLS], a_list[:])
+        gather_vector(got_a[3][:], a_odd[:, A_COLS:], a_list[:])
+        scatter_product(win_1[1], b_list, 1, got_a[1])
         store(out_1, win_1, 1)
+        scatter_half(win_1[2], b_list, values[3][:], 1)
         store(out_1, win_1, 2)
+        scatter_product(win_1[3], b_list, 3, got_a[3])
+        store(out_1, win_1, 3)

@@ -125,8 +125,8 @@ def tile_attend_gqr_ab_kernel(tc, aT, bT, W, dz, offs, joffs, out_0, out_1):
         def scatter_product(window, entries, t, gathered):
             nc.vector.tensor_tensor(window[:].indirect(entries[:]), de[t][:], gathered[:], MULT)
 
-        def store(out, wins, t):
-            nc.sync.dma_start(out=out[rows(t), :], in_=wins[t][:])
+        def store(out, wins, t, queue=nc.sync):
+            queue.dma_start(out=out[rows(t), :], in_=wins[t][:])
 
         w_rows = W.rearrange("(p t) d -> p t d", t=PACK)
         nc.sync.dma_start(out=dz_raw[:], in_=dz.rearrange("(p t) i -> p t i", t=PACK))
@@ -184,7 +184,7 @@ def tile_attend_gqr_ab_kernel(tc, aT, bT, W, dz, offs, joffs, out_0, out_1):
         product(values[0][:], de_half(2, 0), got[:, 0:HALF])
         scatter_half(win_0[2], a_list, values[0][:], 0)
         scatter_product(win_0[3], a_list, 3, got_b[3])
-        store(out_0, win_0, 3)
+        store(out_0, win_0, 3, nc.gpsimd)
 
         gather_scalar(got[:, ITEMS : 2 * ITEMS], a_even[:, 0:A_COLS], a_list[:])
         gather_scalar(got[:, 2 * ITEMS :], a_even[:, A_COLS:], half_of(a_list, 0))
@@ -193,7 +193,7 @@ def tile_attend_gqr_ab_kernel(tc, aT, bT, W, dz, offs, joffs, out_0, out_1):
         product(values[2][:], mixed[1][:], got[:, 3 * HALF : 5 * HALF])
         product(values[3][:], de_half(2, 1), got[:, half(1)])
         scatter_half(win_0[2], a_list, values[1][:, half(0)], 1)
-        store(out_0, win_0, 2)
+        store(out_0, win_0, 2, nc.gpsimd)
         scatter_half(win_1[0], b_list, values[1][:, half(1)], 0)
         scatter_half(win_1[2], b_list, values[2][:, half(1)], 0)
         scatter_half(win_1[0], b_list, values[2][:, half(0)], 1)

@@ -197,13 +197,13 @@ def tile_attend_gqr_ab_kernel(tc, aT, bT, W, dz, offs, joffs, out_0, out_1):
         scatter_half(win_1[0], b_list, values[1][:, half(1)], 0)
         scatter_half(win_1[2], b_list, values[2][:, half(1)], 0)
         scatter_half(win_1[0], b_list, values[2][:, half(0)], 1)
-        store(out_1, win_1, 0)
+        store(out_1, win_1, 0, nc.scalar)
 
         gather_vector(got_a[1][:], a_odd[:, 0:A_COLS], a_list[:])
         gather_vector(got_a[3][:], a_odd[:, A_COLS:], a_list[:])
         scatter_product(win_1[1], b_list, 1, got_a[1])
         store(out_1, win_1, 1)
         scatter_half(win_1[2], b_list, values[3][:], 1)
-        store(out_1, win_1, 2)
+        store(out_1, win_1, 2, nc.scalar)
         scatter_product(win_1[3], b_list, 3, got_a[3])
         store(out_1, win_1, 3)

from contextlib import ExitStack

import concourse.mybir as mybir

D, F, ITEMS, A_COLS, B_COLS = 512, 512, 512, 2048, 1024
FLOPS = 2 * D * F * ITEMS

F32 = mybir.dt.float32
BF16 = mybir.dt.bfloat16
U32 = mybir.dt.uint32
I32 = mybir.dt.int32
U16 = mybir.dt.uint16
U8 = mybir.dt.uint8
E4M3X4 = mybir.dt.float8_e4m3fn_x4
E5M2X4 = mybir.dt.float8_e5m2_x4
MULT = mybir.AluOpType.mult
COPY = mybir.ActivationFunctionType.Copy

P = 128
PACK = 4
D_TILES = D // P
HALF = ITEMS // 2
PAIR = 2 * P
LIST_STRIPE = 16
KIB = 1024
SPLIT = 352


def interleave(copy, grouped, raw):
    copy(
        out=grouped.rearrange("p (c i t) -> p c t i", i=PACK, t=PACK),
        in_=raw.rearrange("p t (c i) -> p c t i", i=PACK),
    )


def tile_attend_gqr_ab_kernel(tc, aT, bT, W, dz, offs, joffs, out_0, out_1):
    nc = tc.nc
    with ExitStack() as ctx:
        keep = ctx.enter_context(tc.tile_pool(name="keep", bufs=1))
        shared = ctx.enter_context(tc.tile_pool(name="shared", bufs=1))
        psum = ctx.enter_context(tc.psum_pool(name="psum", bufs=1))

        def on(name, shape, dtype, at):
            return shared.tile(shape, dtype, name=name, align_bytes=64, offset=at)

        a_list = keep.tile([P, ITEMS // LIST_STRIPE], U16, name="a_list")
        b_list = keep.tile([P, ITEMS // LIST_STRIPE], U16, name="b_list")
        dz_raw = keep.tile([P, PACK, ITEMS], F32, name="dz_raw")
        w_raw = [keep.tile([P, PACK, PAIR], F32, name=f"w_raw{h}") for h in range(2)]
        a_even = keep.tile([P, 2 * A_COLS], F32, name="a_even")
        a_odd = keep.tile([P, 2 * A_COLS], F32, name="a_odd")
        b_0 = keep.tile([P, B_COLS], F32, name="b_0")
        b_1 = on("b_1", [P, B_COLS], F32, 20 * KIB)
        b_pair = keep.tile([P, 2 * B_COLS], F32, name="b_pair")
        win_0 = {t: keep.tile([P, A_COLS], F32, name=f"win_0_{t}") for t in (0, 1, 3)}
        win_0 = [win_0[0], win_0[1], on("win_0_2", [P, A_COLS], F32, 0), win_0[3]]
        win_1 = [on(f"win_1_{t}", [P, B_COLS], F32, at * KIB) for t, at in enumerate((22, 18, 8, 12))]
        dz_bf = keep.tile([P, ITEMS * PACK], BF16, name="dz_bf", align_bytes=64)
        w_bf = [keep.tile([P, PAIR * PACK], BF16, name="w_bf0", align_bytes=64)]
        w_bf.append(on("w_bf1", [P, PAIR * PACK], BF16, 7 * KIB))
        dz_codes = keep.tile([P, ITEMS], U32, name="dz_codes", align_bytes=64)
        dz_scales = keep.tile([P, ITEMS], U8, name="dz_scales", align_bytes=64)
        w_codes = [keep.tile([P, PAIR], U32, name="w_codes0", align_bytes=64)]
        w_codes.append(on("w_codes1", [P, PAIR], U32, 21 * KIB + KIB // 2))
        w_scales = [keep.tile([P, PAIR], U8, name="w_scales0", align_bytes=64)]
        w_scales.append(on("w_scales1", [P, PAIR], U8, 12 * KIB))
        de = {1: on("de1", [P, ITEMS], F32, 48 * KIB), 3: keep.tile([P, ITEMS], F32, name="de3")}
        got_first = [keep.tile([P, HALF], F32, name="got_first0"), on("got_first1", [P, HALF], F32, 48 * KIB)]
        got = keep.tile([P, 5 * HALF], F32, name="got")
        got_b = {t: keep.tile([P, ITEMS], F32, name=f"got_b{t}") for t in (1, 3)}
        got_a = {t: keep.tile([P, ITEMS], F32, name=f"got_a{t}") for t in (1, 3)}
        first = [keep.tile([P, HALF], F32, name=f"first{h}") for h in range(2)]
        values = [keep.tile([P, HALF], F32, name="values0"), keep.tile([P, ITEMS], F32, name="values1")]
        values = values + [keep.tile([P, ITEMS], F32, name="values2"), keep.tile([P, HALF], F32, name="values3")]
        whole = {t: psum.tile([P, ITEMS], F32, name=f"bank{t}") for t in (1, 3)}
        mixed = [psum.tile([P, ITEMS], F32, name=f"mixed{h}") for h in range(2)]

        def rows(t):
            return slice(t * P, (t + 1) * P)

        def half(h):
            return slice(h * HALF, (h + 1) * HALF)

        def part(entries, first_item, last_item):
            return entries[:, first_item // LIST_STRIPE : last_item // LIST_STRIPE]

        def half_of(entries, h):
            return part(entries, h * HALF, (h + 1) * HALF)

        def cast(copy, grouped, raw, first_col, last_col):
            interleave(copy, grouped[:, PACK * first_col : PACK * last_col], raw[:, :, first_col:last_col])

        def quantize_w(h):
            nc.vector.quantize_mx(out=w_codes[h][:].bitcast(E4M3X4), scales=w_scales[h][:], in_=w_bf[h][:])

        def multiply(out, t, items):
            nc.tensor.matmul_mx(
                out=out,
                lhsT=w_codes[t // 2][:, rows(t % 2)].bitcast(E4M3X4),
                lhsT_scale=w_scales[t // 2][:, rows(t % 2)],
                rhs=dz_codes[:, items].bitcast(E5M2X4),
                rhs_scale=dz_scales[:, items],
                start=True,
                stop=True,
            )

        def de_half(t, h):
            return mixed[(t // 2 + h) % 2][:, half(1 - h)]

        def clear(window):
            nc.gpsimd.memset(window[:].bitcast(I32), 0)

        def gather_scalar(out, table, entries):
            nc.scalar.activation(out, table.indirect(entries), COPY)

        def gather_vector(out, table, entries):
            nc.vector.tensor_copy(out, table.indirect(entries))

        def product(out, bank, gathered):
            nc.vector.tensor_tensor(out, bank, gathered, MULT)

        def scatter_half(window, entries, vals, h):
            nc.scalar.activation(window[:].indirect(half_of(entries, h)), vals, COPY)

        def scatter_product(window, entries, t, gathered):
            nc.vector.tensor_tensor(window[:].indirect(entries[:]), de[t][:], gathered[:], MULT)

        def store(out, wins, t, queue=nc.sync):
            queue.dma_start(out=out[rows(t), :], in_=wins[t][:])

        w_rows = W.rearrange("(p t) d -> p t d", t=PACK)
        nc.sync.dma_start(out=dz_raw[:], in_=dz.rearrange("(p t) i -> p t i", t=PACK))
        nc.sync.dma_start(out=w_raw[0][:], in_=w_rows[:, :, half(0)])
        nc.sync.dma_start(b_list[:], joffs)
        nc.sync.dma_start(out=b_0[:], in_=bT[rows(0), :])
        nc.sync.dma_start(a_list[:], offs)
        nc.sync.dma_start(out=w_raw[1][:], in_=w_rows[:, :, half(1)])
        nc.sync.dma_start(out=b_1[:], in_=bT[rows(1), :])
        nc.sync.dma_start(
            out=b_pair[:].rearrange("p (t c) -> p t c", t=2), in_=bT[PAIR:D, :].rearrange("(t p) c -> p t c", t=2)
        )
        a_rows = aT.rearrange("(u t p) c -> t p u c", u=2, t=2)
        for t, pair in enumerate((a_even, a_odd)):
            nc.sync.dma_start(out=pair[:].rearrange("p (u c) -> p u c", u=2), in_=a_rows[t])

        for t in (0, 1, 3):
            nc.vector.memset(win_0[t][:].bitcast(I32), 0)

        cast(nc.scalar.copy, dz_bf, dz_raw, 0, 192)
        cast(nc.vector.tensor_copy, dz_bf, dz_raw, 192, ITEMS)
        cast(nc.vector.tensor_copy, w_bf[0], w_raw[0], 0, 160)
        cast(nc.scalar.copy, w_bf[0], w_raw[0], 160, PAIR)
        nc.vector.quantize_mx(out=dz_codes[:].bitcast(E5M2X4), scales=dz_scales[:], in_=dz_bf[:])
        quantize_w(0)
        for h in range(2):
            multiply(de_half(0, h), 0, half(h))
        multiply(whole[1][:], 1, slice(0, ITEMS))

        gather_scalar(got_first[0][:], b_0[:], half_of(b_list, 0))
        gather_vector(got_first[1][:], b_0[:], half_of(b_list, 1))
        for h in range(2):
            product(first[h][:], de_half(0, h), got_first[h][:])
        scatter_half(win_0[0], a_list, first[0][:], 0)
        nc.scalar.copy(out=de[1][:], in_=whole[1][:])
        scatter_half(win_0[0], a_list, first[1][:], 1)
        store(out_0, win_0, 0)

        cast(nc.vector.tensor_copy, w_bf[1], w_raw[1], 0, PAIR)
        gather_vector(got_b[1][:], b_1[:], b_list[:])
        quantize_w(1)
        multiply(whole[3][:], 3, slice(0, ITEMS))
        for h in range(2):
            multiply(de_half(2, h), 2, half(h))
        clear(win_0[2])
        for t in (1, 0, 2, 3):
            clear(win_1[t])
        scatter_product(win_0[1], a_list, 1, got_b[1])
        store(out_0, win_0, 1)

        nc.scalar.copy(out=de[3][:], in_=whole[3][:])
        gather_scalar(got[:, 0:ITEMS], b_pair[:, 0:B_COLS], b_list[:])
        gather_scalar(got_b[3][:, 0:SPLIT], b_pair[:, B_COLS:], part(b_list, 0, SPLIT))
        gather_vector(got_b[3][:, SPLIT:], b_pair[:, B_COLS:], part(b_list, SPLIT, ITEMS))
        product(values[0][:], de_half(2, 0), got[:, 0:HALF])
        scatter_half(win_0[2], a_list, values[0][:], 0)
        scatter_product(win_0[3], a_list, 3, got_b[3])
        store(out_0, win_0, 3, nc.gpsimd)

        gather_scalar(got[:, ITEMS : 2 * ITEMS], a_even[:, 0:A_COLS], a_list[:])
        gather_scalar(got[:, 2 * ITEMS :], a_even[:, A_COLS:], half_of(a_list, 0))
        product(values[1][:], mixed[0][:], got[:, HALF : 3 * HALF])
        gather_vector(got[:, half(1)], a_even[:, A_COLS:], half_of(a_list, 1))
        product(values[2][:], mixed[1][:], got[:, 3 * HALF : 5 * HALF])
        product(values[3][:], de_half(2, 1), got[:, half(1)])
        scatter_half(win_0[2], a_list, values[1][:, half(0)], 1)
        store(out_0, win_0, 2, nc.gpsimd)
        scatter_half(win_1[0], b_list, values[1][:, half(1)], 0)
        scatter_half(win_1[2], b_list, values[2][:, half(1)], 0)
        scatter_half(win_1[0], b_list, values[2][:, half(0)], 1)
        store(out_1, win_1, 0, nc.scalar)

        gather_vector(got_a[1][:], a_odd[:, 0:A_COLS], a_list[:])
        gather_vector(got_a[3][:], a_odd[:, A_COLS:], a_list[:])
        scatter_product(win_1[1], b_list, 1, got_a[1])
        store(out_1, win_1, 1)
        scatter_half(win_1[2], b_list, values[3][:], 1)
        store(out_1, win_1, 2, nc.scalar)
        scatter_product(win_1[3], b_list, 3, got_a[3])
        store(out_1, win_1, 3)
